import numpy as np
import ml_dtypes


def mxq(x, axis, fmt="e4m3"):
    dtype, down = {"e4m3": (ml_dtypes.float8_e4m3fn, 7), "e5m2": (ml_dtypes.float8_e5m2, 14)}[fmt]
    v = np.moveaxis(np.asarray(x, np.float32).astype(ml_dtypes.bfloat16).astype(np.float64), axis, -1)
    blocks = v.reshape(v.shape[:-1] + (-1, 32))
    amax = np.abs(blocks).max(-1, keepdims=True)
    byte = np.maximum(np.where(amax > 0, np.frexp(amax)[1] - 1 + 127, 0) - down, 1)
    scale = np.exp2(byte - 127.0)
    codes = (blocks / scale).astype(np.float32).astype(dtype).astype(np.float64)
    return np.moveaxis((codes * scale).reshape(v.shape), -1, axis)


WIDE = False


def mx_kscale(k):
    if not WIDE:
        return np.ones(k)
    levels = np.array([10, -10, 5, -5, 0])
    if k % 512:
        return np.exp2(np.random.permutation(np.resize(levels, k // 32))).repeat(32)
    a = np.empty((k // 512, 16))
    for p in range(k // 512):
        a[p, :8] = np.random.permutation(np.resize(levels, 8))
        for g in range(8):
            far = levels[np.abs(levels - a[p, g]) >= 10]
            a[p, g + 8] = far[np.random.randint(len(far))]
    return np.exp2(a.ravel()).repeat(32)


def f64(x):
    return np.asarray(x).astype(np.float64)


def striped(idx):
    return np.tile(idx.reshape(-1, 16).T, (8, 1)).astype(np.uint16)


def unstriped(offs):
    return offs[:16].T.reshape(-1).astype(np.int64)


def striped8(idx):
    return np.concatenate([x.reshape(-1, 16).T for x in idx]).astype(np.uint16)


def runs(offs, k):
    lists = np.stack([offs[16 * r : 16 * r + 16].T.reshape(-1) for r in range(8)]).astype(np.int64)
    return lists[np.arange(k) % 512 // 64]


def pack_weight(w):
    k, n = w.shape
    w = f64(np.asarray(w, np.float32).astype(ml_dtypes.bfloat16)).reshape(k // 32, 32, n)
    amax = np.abs(w).max(1)
    byte = np.clip(np.where(amax > 0, np.frexp(amax)[1] - 1 + 127 - 7, 1), 1, 254)
    scaled = (w * np.exp2(127.0 - byte)[:, None, :]).reshape(k, n).astype(np.float32)
    words = np.ascontiguousarray(scaled.reshape(k // 512, 128, 4, n).transpose(0, 1, 3, 2)).astype(ml_dtypes.float8_e4m3fn).view(np.uint8)
    return words, np.ascontiguousarray(byte.astype(np.uint8).reshape(k // 512, 16, n))


def unpack_weight(words, scales):
    g, p, n, _ = words.shape
    vals = np.ascontiguousarray(words).view(ml_dtypes.float8_e4m3fn).astype(np.float64) * np.repeat(np.exp2(scales.astype(np.float64) - 127.0), 8, axis=1)[..., None]
    return vals.transpose(0, 1, 3, 2).reshape(g * 512, n)


K, T, S, N, G, H = 512, 2048, 512, 512, 2048, 512


def setup_inputs():
    n = np.random.standard_normal
    s = mx_kscale(K)[:, None]
    u = mx_kscale(H)
    packed_xT = pack_weight(n((K, T)) * s)
    packed_dT = pack_weight(n((K, G)) / s)
    return {
        "x_words": packed_xT[0],
        "x_scales": packed_xT[1],
        "d_words": packed_dT[0],
        "d_scales": packed_dT[1],
        "gn": (np.random.uniform(0.5, 1.5, (H, 1)) * u[:, None]).astype(np.float32),
        "w1": (n((H, N)) / np.sqrt(H) / u[:, None]).astype(np.float32),
        "offs": striped(np.random.permutation(T)[:S]),
        "kidx": striped8(np.random.randint(0, G, (8, H))),
        "nb": striped8(np.stack([np.random.permutation(S) for _ in range(8)])),
    }


def reference(x_words, x_scales, d_words, d_scales, gn, w1, offs, kidx, nb):
    d_kidx = unpack_weight(d_words, d_scales)[np.arange(K)[:, None], runs(kidx, K)]
    xq = unpack_weight(x_words, x_scales)[:, unstriped(offs)]
    s = 0.03125 * (d_kidx.T @ xq)
    e = np.exp(s - s.max(axis=1, keepdims=True))
    p = e / e.sum(axis=1, keepdims=True)
    z = f64(gn) * (32.0 * (p + p[np.arange(H)[:, None], runs(nb, H)]))
    return mxq(f64(w1), 0, "e4m3").T @ mxq(z, 0, "e4m3")

@@ -1,0 +1,154 @@
+from contextlib import ExitStack
+
+import concourse.mybir as mybir
+
+F32 = mybir.dt.float32
+BF16 = mybir.dt.bfloat16
+I32 = mybir.dt.int32
+U32 = mybir.dt.uint32
+U16 = mybir.dt.uint16
+U8 = mybir.dt.uint8
+FP8X4 = mybir.dt.float8_e4m3fn_x4
+ALU = mybir.AluOpType
+ACT = mybir.ActivationFunctionType
+
+P = 128
+PACK = 4
+K, T, S, N, G, H = 512, 2048, 512, 512, 2048, 512
+FLOPS = 2 * K * H * S + 2 * H * N * S
+LIST = 16
+
+
+def interleave(engine_copy, dst, src):
+    engine_copy(dst.rearrange("p (c i) t -> p c t i", i=PACK), src.rearrange("p t (c i) -> p c t i", i=PACK))
+
+
+def tile_picked_softkeys_none_p_kernel(
+    tc, x_words, x_scales, d_words, d_scales, gn, w1, offs, kidx, nb, out
+):
+    nc = tc.nc
+    with ExitStack() as ctx:
+        keep = ctx.enter_context(tc.tile_pool(name="keep", bufs=1))
+        psum = ctx.enter_context(tc.psum_pool(name="psum", bufs=1))
+
+        kidx_sb = keep.tile([P, H // LIST], U16, name="kidx_sb")
+        offs_sb = keep.tile([P, S // LIST], U16, name="offs_sb")
+        nb_sb = keep.tile([P, S // LIST], U16, name="nb_sb")
+        dsc_tab = keep.tile([P, G], U8, name="dsc_tab", align_bytes=64)
+        xsc_tab = keep.tile([P, T], U8, name="xsc_tab", align_bytes=64)
+        dw_tab = keep.tile([P, G], U32, name="dw_tab", align_bytes=64)
+        xw_tab = keep.tile([P, T], U32, name="xw_tab", align_bytes=64)
+        dsc = keep.tile([P, H], U8, name="dsc", align_bytes=64)
+        gn_sb = keep.tile([P, PACK], F32, name="gn_sb")
+        warm = keep.tile([P, 1], F32, name="warm")
+        warm2 = keep.tile([P, 1], F32, name="warm2")
+
+        nc.vector.memset(dsc_tab[:].bitcast(I32), 0)
+        nc.vector.memset(xsc_tab[:].bitcast(I32), 0)
+        nc.vector.memset(warm[:], 0.0)
+        nc.vector.memset(dsc[:].bitcast(I32), 0)
+
+        d_rows = d_words[0].rearrange("p n t -> p (n t)").bitcast(I32)
+        LEAD = 512
+        nc.sync.dma_start(kidx_sb[:], kidx)
+        nc.sync.dma_start(dw_tab[:, 0:LEAD].bitcast(I32), d_rows[:, 0:LEAD])
+        nc.sync.dma_start(dsc_tab[0:P:8, :].bitcast(I32), d_scales[0].bitcast(I32))
+        nc.sync.dma_start(dw_tab[:, LEAD:G].bitcast(I32), d_rows[:, LEAD:G])
+        nc.sync.dma_start(offs_sb[:], offs)
+        for a in range(4):
+            nc.scalar.dma_start(xsc_tab[a:P:32, :].bitcast(I32), x_scales[0][a:16:4, :].bitcast(I32))
+        nc.sync.dma_start(xw_tab[:].bitcast(I32), x_words[0].rearrange("p n t -> p (n t)").bitcast(I32))
+        nc.sync.dma_start(nb_sb[:], nb)
+        nc.gpsimd.dma_start(gn_sb[:], gn.rearrange("(p t) o -> p (t o)", t=PACK))
+        nc.scalar.activation(warm2[:], warm[:], ACT.Exp)
+
+        dsc_g = keep.tile([P, H], U8, name="dsc_g", align_bytes=64)
+        dsc_p = keep.tile([P, H], U8, name="dsc_p", tag="staging", align_bytes=64)
+        nc.vector.tensor_copy(dsc_g[:], dsc_tab[:].indirect(kidx_sb[:]))
+        nc.vector.tensor_copy(dsc_p[:].rearrange("p (t m) -> p m t", t=PACK), dsc_g[:].rearrange("p (m t) -> p m t", t=PACK))
+        for a in range(4):
+            nc.scalar.dma_start(dsc[a:P:32, :].bitcast(I32), dsc_p[8 * a : P : 32, :].bitcast(I32))
+        w_raw = keep.tile([P, 2, PACK, N // 2], F32, name="w_raw", tag="staging", align_bytes=64)
+        for h in range(2):
+            nc.sync.dma_start(w_raw[:, h], w1[:, h * (N // 2) : (h + 1) * (N // 2)].rearrange("(p t) m -> p t m", t=PACK))
+        xsc = keep.tile([P, S], U8, name="xsc", align_bytes=64)
+        dw_g = keep.tile([P, H], U32, name="dw_g", align_bytes=64)
+        dw = keep.tile([P, H], U32, name="dw", align_bytes=64)
+        xw = keep.tile([P, S], U32, name="xw", align_bytes=64)
+        nc.vector.tensor_copy(xsc[:], xsc_tab[:].indirect(offs_sb[:]))
+        nc.vector.tensor_copy(dw_g[:], dw_tab[:].indirect(kidx_sb[:]))
+        nc.vector.tensor_copy(dw[:].rearrange("p (t m) -> p m t", t=PACK), dw_g[:].rearrange("p (m t) -> p m t", t=PACK))
+        nc.vector.tensor_copy(xw[:], xw_tab[:].indirect(offs_sb[:]))
+
+        neg, low, e, tot, rec, c, win, plain = [], [], [], [], [], [], [], []
+        for t in range(PACK):
+            bank = psum.tile([P, S], F32, name=f"score{t}")
+            cols = slice(t * P, (t + 1) * P)
+            nc.tensor.matmul_mx(out=bank[:], lhsT=dw[:, cols].bitcast(FP8X4), lhsT_scale=dsc[:, cols],
+                                rhs=xw[:].bitcast(FP8X4), rhs_scale=xsc[:], start=True, stop=True)
+            neg.append(keep.tile([P, S], F32, name=f"neg{t}"))
+            low.append(keep.tile([P, 1], F32, name=f"low{t}"))
+            nc.vector.tensor_scalar(neg[t][:], bank[:], -0.03125, None, ALU.mult, ALU.min, accum_out=low[t][:])
+        w_grp = keep.tile([P, N, PACK], BF16, name="w_grp", align_bytes=64)
+        w_codes = keep.tile([P, N], U32, name="w_codes", align_bytes=64)
+        w_sc = keep.tile([P, N], U8, name="w_sc", align_bytes=64)
+        HALF = S // 2
+        zsum = [keep.tile([P, PACK, HALF], F32, name=f"zsum{h}") for h in range(2)]
+
+        def softmax(t):
+            e.append(keep.tile([P, S], F32, name=f"e{t}"))
+            tot.append(keep.tile([P, 1], F32, name=f"tot{t}"))
+            rec.append(keep.tile([P, 1], F32, name=f"rec{t}"))
+            c.append(keep.tile([P, 1], F32, name=f"c{t}"))
+            win.append(keep.tile([P, S], F32, name=f"win{t}"))
+            plain.append(keep.tile([P, S], F32, name=f"plain{t}"))
+            nc.scalar.activation(e[t][:], neg[t][:], ACT.Exp, bias=low[t][:], scale=-1.0, accum_out=tot[t][:])
+            nc.vector.reciprocal(rec[t][:], tot[t][:])
+            nc.vector.tensor_scalar(c[t][:], rec[t][:], gn_sb[:, t : t + 1], 32.0, ALU.mult, ALU.mult)
+            nc.scalar.activation(win[t][:], e[t][:], ACT.Copy, scale=c[t][:])
+            nc.vector.tensor_scalar(plain[t][:], e[t][:], c[t][:], None, ALU.mult)
+
+        def gather(t, h):
+            cols = slice(h * HALF, (h + 1) * HALF)
+            nc.vector.tensor_tensor(zsum[h][:, t, :], win[t][:].indirect(nb_sb[:, h * HALF // LIST : (h + 1) * HALF // LIST]), plain[t][:, cols], ALU.add)
+
+        def gp_copy(dst, src):
+            nc.gpsimd.tensor_scalar(dst, src, 1.0, 0.0, ALU.mult, ALU.add)
+
+        for t in range(PACK):
+            softmax(t)
+            if t < 2:
+                gather(t, 0)
+                gather(t, 1)
+            else:
+                gather(t, 0)
+        for q in range(4):
+            WQ = N // 4
+            interleave(nc.scalar.copy, w_grp[:, q * WQ : (q + 1) * WQ, :], w_raw[:, q * WQ // (N // 2), :, q * WQ % (N // 2) : q * WQ % (N // 2) + WQ])
+        z_grp = [keep.tile([P, HALF, PACK], BF16, name=f"z_grp{h}", align_bytes=64) for h in range(2)]
+        z_codes = [keep.tile([P, HALF], U32, name=f"z_codes{h}", align_bytes=64) for h in range(2)]
+        z_sc = [keep.tile([P, HALF], U8, name=f"z_sc{h}", align_bytes=64) for h in range(2)]
+        interleave(nc.scalar.copy, z_grp[0][:], zsum[0][:])
+        gather(2, 1)
+        nc.vector.quantize_mx(out=w_codes[:].bitcast(FP8X4), scales=w_sc[:], in_=w_grp[:].rearrange("p m t -> p (m t)"))
+        gather(3, 1)
+
+        def finish(h):
+            nc.vector.quantize_mx(out=z_codes[h][:].bitcast(FP8X4), scales=z_sc[h][:], in_=z_grp[h][:].rearrange("p j t -> p (j t)"))
+            for b in range(2):
+                acc = psum.tile([P, 2, HALF], F32, name=f"acc{h}{b}")
+                for u in range(2):
+                    cols = slice((2 * b + u) * P, (2 * b + u + 1) * P)
+                    nc.tensor.matmul_mx(out=acc[:, u, :], lhsT=w_codes[:, cols].bitcast(FP8X4), lhsT_scale=w_sc[:, cols],
+                                        rhs=z_codes[h][:].bitcast(FP8X4), rhs_scale=z_sc[h][:], start=True, stop=True)
+                res = keep.tile([P, 2, HALF], F32, name=f"res{h}{b}")
+                if h == 1 and b == 1:
+                    nc.vector.tensor_copy(res[:], acc[:])
+                else:
+                    nc.scalar.copy(res[:], acc[:])
+                nc.sync.dma_start(out[2 * b * P : (2 * b + 2) * P, h * HALF : (h + 1) * HALF].rearrange("(u p) j -> p u j", p=P), res[:])
+
+        finish(0)
+        interleave(nc.vector.tensor_copy, z_grp[1][:, 0:176, :], zsum[1][:, :, 0:176])
+        interleave(nc.scalar.copy, z_grp[1][:, 176:HALF, :], zsum[1][:, :, 176:HALF])
+        finish(1)

@@ -12,15 +12,33 @@ FP8X4 = mybir.dt.float8_e4m3fn_x4
 ALU = mybir.AluOpType
 ACT = mybir.ActivationFunctionType
 
-P = 128
-PACK = 4
 K, T, S, N, G, H = 512, 2048, 512, 512, 2048, 512
 FLOPS = 2 * K * H * S + 2 * H * N * S
-LIST = 16
+
+P = 128
+SLOTS = 4
+PER_COLUMN = 16
+QUADRANT = 32
+BLOCK = 8
+RUN = 4
+SCORE_SCALE = 0.03125
+SHARE_SCALE = 32.0
+LEAD = 512
+W_HALF = N // 2
+X_HALF = S // 2
+CHUNKS = (256, 128, 128)
 
 
-def interleave(engine_copy, dst, src):
-    engine_copy(dst.rearrange("p (c i) t -> p c t i", i=PACK), src.rearrange("p t (c i) -> p c t i", i=PACK))
+def side_by_side(grouped):
+    return grouped.rearrange("p (c i) t -> p c t i", i=RUN)
+
+
+def by_slot(planes):
+    return planes.rearrange("p t (c i) -> p c t i", i=RUN)
+
+
+def entries(offsets, start, count):
+    return offsets[:, start // PER_COLUMN : (start + count) // PER_COLUMN]
 
 
 def tile_picked_softkeys_none_p_kernel(
@@ -31,124 +49,178 @@ def tile_picked_softkeys_none_p_kernel(
         keep = ctx.enter_context(tc.tile_pool(name="keep", bufs=1))
         psum = ctx.enter_context(tc.psum_pool(name="psum", bufs=1))
 
-        kidx_sb = keep.tile([P, H // LIST], U16, name="kidx_sb")
-        offs_sb = keep.tile([P, S // LIST], U16, name="offs_sb")
-        nb_sb = keep.tile([P, S // LIST], U16, name="nb_sb")
-        dsc_tab = keep.tile([P, G], U8, name="dsc_tab", align_bytes=64)
-        xsc_tab = keep.tile([P, T], U8, name="xsc_tab", align_bytes=64)
-        dw_tab = keep.tile([P, G], U32, name="dw_tab", align_bytes=64)
-        xw_tab = keep.tile([P, T], U32, name="xw_tab", align_bytes=64)
-        dsc = keep.tile([P, H], U8, name="dsc", align_bytes=64)
-        gn_sb = keep.tile([P, PACK], F32, name="gn_sb")
-        warm = keep.tile([P, 1], F32, name="warm")
-        warm2 = keep.tile([P, 1], F32, name="warm2")
+        kidx_sb = keep.tile([P, H // PER_COLUMN], U16, name="kidx_sb")
+        offs_sb = keep.tile([P, S // PER_COLUMN], U16, name="offs_sb")
+        nb_sb = keep.tile([P, S // PER_COLUMN], U16, name="nb_sb")
+        d_scale_table = keep.tile([P, G], U8, name="d_scale_table", align_bytes=64)
+        x_scale_table = keep.tile([P, T], U8, name="x_scale_table", align_bytes=64)
+        d_word_table = keep.tile([P, G], U32, name="d_word_table", tag="d_word_table", align_bytes=64)
+        x_word_table = keep.tile([P, T], U32, name="x_word_table", tag="x_word_table", align_bytes=64)
+        key_scales = keep.tile([P, H], U8, name="key_scales", align_bytes=64)
+        gn_sb = keep.tile([P, SLOTS], F32, name="gn_sb")
+        warm_in = keep.tile([P, 1], F32, name="warm_in")
+        warm_out = keep.tile([P, 1], F32, name="warm_out")
 
-        nc.vector.memset(dsc_tab[:].bitcast(I32), 0)
-        nc.vector.memset(xsc_tab[:].bitcast(I32), 0)
-        nc.vector.memset(warm[:], 0.0)
-        nc.vector.memset(dsc[:].bitcast(I32), 0)
+        nc.vector.memset(d_scale_table[:].bitcast(I32), 0)
+        nc.vector.memset(x_scale_table[:].bitcast(I32), 0)
+        nc.vector.memset(warm_in[:], 0.0)
+        nc.vector.memset(key_scales[:].bitcast(I32), 0)
 
         d_rows = d_words[0].rearrange("p n t -> p (n t)").bitcast(I32)
-        LEAD = 512
         nc.sync.dma_start(kidx_sb[:], kidx)
-        nc.sync.dma_start(dw_tab[:, 0:LEAD].bitcast(I32), d_rows[:, 0:LEAD])
-        nc.sync.dma_start(dsc_tab[0:P:8, :].bitcast(I32), d_scales[0].bitcast(I32))
-        nc.sync.dma_start(dw_tab[:, LEAD:G].bitcast(I32), d_rows[:, LEAD:G])
+        nc.sync.dma_start(d_word_table[:, 0:LEAD].bitcast(I32), d_rows[:, 0:LEAD])
+        nc.sync.dma_start(d_scale_table[0:P:BLOCK, :].bitcast(I32), d_scales[0].bitcast(I32))
+        nc.sync.dma_start(d_word_table[:, LEAD:G].bitcast(I32), d_rows[:, LEAD:G])
         nc.sync.dma_start(offs_sb[:], offs)
         for a in range(4):
-            nc.scalar.dma_start(xsc_tab[a:P:32, :].bitcast(I32), x_scales[0][a:16:4, :].bitcast(I32))
-        nc.sync.dma_start(xw_tab[:].bitcast(I32), x_words[0].rearrange("p n t -> p (n t)").bitcast(I32))
+            nc.scalar.dma_start(x_scale_table[a:P:QUADRANT, :].bitcast(I32), x_scales[0][a : P // BLOCK : 4, :].bitcast(I32))
+        nc.sync.dma_start(x_word_table[:].bitcast(I32), x_words[0].rearrange("p n t -> p (n t)").bitcast(I32))
         nc.sync.dma_start(nb_sb[:], nb)
-        nc.gpsimd.dma_start(gn_sb[:], gn.rearrange("(p t) o -> p (t o)", t=PACK))
-        nc.scalar.activation(warm2[:], warm[:], ACT.Exp)
+        nc.gpsimd.dma_start(gn_sb[:], gn.rearrange("(p t) o -> p (t o)", t=SLOTS))
+        nc.scalar.activation(warm_out[:], warm_in[:], ACT.Exp)
 
-        dsc_g = keep.tile([P, H], U8, name="dsc_g", align_bytes=64)
-        dsc_p = keep.tile([P, H], U8, name="dsc_p", tag="staging", align_bytes=64)
-        nc.vector.tensor_copy(dsc_g[:], dsc_tab[:].indirect(kidx_sb[:]))
-        nc.vector.tensor_copy(dsc_p[:].rearrange("p (t m) -> p m t", t=PACK), dsc_g[:].rearrange("p (m t) -> p m t", t=PACK))
+        picked_scales = keep.tile([P, H], U8, name="picked_scales", tag="picked_scales", align_bytes=64)
+        dealt_scales = keep.tile([P, H], U8, name="dealt_scales", align_bytes=64)
+        nc.vector.tensor_copy(picked_scales[:], d_scale_table[:].indirect(kidx_sb[:]))
+        nc.vector.tensor_copy(
+            dealt_scales[:].rearrange("p (t m) -> p m t", t=SLOTS), picked_scales[:].rearrange("p (m t) -> p m t", t=SLOTS)
+        )
         for a in range(4):
-            nc.scalar.dma_start(dsc[a:P:32, :].bitcast(I32), dsc_p[8 * a : P : 32, :].bitcast(I32))
-        w_raw = keep.tile([P, 2, PACK, N // 2], F32, name="w_raw", tag="staging", align_bytes=64)
-        for h in range(2):
-            nc.sync.dma_start(w_raw[:, h], w1[:, h * (N // 2) : (h + 1) * (N // 2)].rearrange("(p t) m -> p t m", t=PACK))
-        xsc = keep.tile([P, S], U8, name="xsc", align_bytes=64)
-        dw_g = keep.tile([P, H], U32, name="dw_g", align_bytes=64)
-        dw = keep.tile([P, H], U32, name="dw", align_bytes=64)
-        xw = keep.tile([P, S], U32, name="xw", align_bytes=64)
-        nc.vector.tensor_copy(xsc[:], xsc_tab[:].indirect(offs_sb[:]))
-        nc.vector.tensor_copy(dw_g[:], dw_tab[:].indirect(kidx_sb[:]))
-        nc.vector.tensor_copy(dw[:].rearrange("p (t m) -> p m t", t=PACK), dw_g[:].rearrange("p (m t) -> p m t", t=PACK))
-        nc.vector.tensor_copy(xw[:], xw_tab[:].indirect(offs_sb[:]))
+            nc.scalar.dma_start(key_scales[a:P:QUADRANT, :].bitcast(I32), dealt_scales[BLOCK * a : P : QUADRANT, :].bitcast(I32))
 
-        neg, low, e, tot, rec, c, win, plain = [], [], [], [], [], [], [], []
-        for t in range(PACK):
-            bank = psum.tile([P, S], F32, name=f"score{t}")
-            cols = slice(t * P, (t + 1) * P)
-            nc.tensor.matmul_mx(out=bank[:], lhsT=dw[:, cols].bitcast(FP8X4), lhsT_scale=dsc[:, cols],
-                                rhs=xw[:].bitcast(FP8X4), rhs_scale=xsc[:], start=True, stop=True)
-            neg.append(keep.tile([P, S], F32, name=f"neg{t}"))
-            low.append(keep.tile([P, 1], F32, name=f"low{t}"))
-            nc.vector.tensor_scalar(neg[t][:], bank[:], -0.03125, None, ALU.mult, ALU.min, accum_out=low[t][:])
-        w_grp = keep.tile([P, N, PACK], BF16, name="w_grp", align_bytes=64)
-        w_codes = keep.tile([P, N], U32, name="w_codes", align_bytes=64)
-        w_sc = keep.tile([P, N], U8, name="w_sc", align_bytes=64)
-        HALF = S // 2
-        zsum = [keep.tile([P, PACK, HALF], F32, name=f"zsum{h}") for h in range(2)]
+        def load_w(half, tile):
+            cols = slice(half * W_HALF, (half + 1) * W_HALF)
+            nc.sync.dma_start(tile[:], w1[:, cols].rearrange("(p t) m -> p t m", t=SLOTS))
+            return tile
 
-        def softmax(t):
-            e.append(keep.tile([P, S], F32, name=f"e{t}"))
-            tot.append(keep.tile([P, 1], F32, name=f"tot{t}"))
-            rec.append(keep.tile([P, 1], F32, name=f"rec{t}"))
-            c.append(keep.tile([P, 1], F32, name=f"c{t}"))
-            win.append(keep.tile([P, S], F32, name=f"win{t}"))
-            plain.append(keep.tile([P, S], F32, name=f"plain{t}"))
-            nc.scalar.activation(e[t][:], neg[t][:], ACT.Exp, bias=low[t][:], scale=-1.0, accum_out=tot[t][:])
-            nc.vector.reciprocal(rec[t][:], tot[t][:])
-            nc.vector.tensor_scalar(c[t][:], rec[t][:], gn_sb[:, t : t + 1], 32.0, ALU.mult, ALU.mult)
-            nc.scalar.activation(win[t][:], e[t][:], ACT.Copy, scale=c[t][:])
-            nc.vector.tensor_scalar(plain[t][:], e[t][:], c[t][:], None, ALU.mult)
+        first_keys = keep.tile([P, P], U32, name="first_keys", align_bytes=64)
+        query_scales = keep.tile([P, S], U8, name="query_scales", align_bytes=64)
+        query_words = keep.tile([P, S], U32, name="query_words", align_bytes=64)
+        nc.vector.tensor_copy(query_scales[:], x_scale_table[:].indirect(offs_sb[:]))
+        w_raw = [load_w(0, keep.tile([P, SLOTS, W_HALF], F32, name="w_raw0", tag="picked_scales", align_bytes=64))]
+        picked_words = keep.tile([P, H], U32, name="picked_words", align_bytes=64)
+        nc.vector.tensor_copy(picked_words[:], d_word_table[:].indirect(kidx_sb[:]))
+        w_raw.append(load_w(1, keep.tile([P, SLOTS, W_HALF], F32, name="w_raw1", tag="d_word_table", align_bytes=64)))
+        picked_by_slot = picked_words[:].rearrange("p (m t) -> p m t", t=SLOTS)
+        nc.vector.tensor_copy(first_keys[:], picked_by_slot[:, :, 0])
+        halves = [slice(0, X_HALF), slice(X_HALF, S)]
+        for cols in halves:
+            nc.vector.tensor_copy(query_words[:, cols], x_word_table[:].indirect(entries(offs_sb, cols.start, X_HALF)))
+        other_keys = keep.tile([P, SLOTS - 1, P], U32, name="other_keys", tag="x_word_table", align_bytes=64)
+        nc.vector.tensor_copy(other_keys[:].rearrange("p t m -> p m t"), picked_by_slot[:, :, 1:SLOTS])
+        key_words = [first_keys[:]] + [other_keys[:, t, :] for t in range(SLOTS - 1)]
 
-        def gather(t, h):
-            cols = slice(h * HALF, (h + 1) * HALF)
-            nc.vector.tensor_tensor(zsum[h][:, t, :], win[t][:].indirect(nb_sb[:, h * HALF // LIST : (h + 1) * HALF // LIST]), plain[t][:, cols], ALU.add)
+        w_scales = [keep.tile([P, W_HALF], U8, name=f"w_scales{h}", align_bytes=64) for h in range(2)]
 
-        def gp_copy(dst, src):
-            nc.gpsimd.tensor_scalar(dst, src, 1.0, 0.0, ALU.mult, ALU.add)
+        def group_w(half, tag):
+            grouped = keep.tile([P, W_HALF, SLOTS], BF16, name=f"w_grouped{half}", tag=tag, align_bytes=64)
+            nc.scalar.copy(side_by_side(grouped[:]), by_slot(w_raw[half][:]))
+            return grouped
 
-        for t in range(PACK):
-            softmax(t)
-            if t < 2:
-                gather(t, 0)
-                gather(t, 1)
-            else:
-                gather(t, 0)
-        for q in range(4):
-            WQ = N // 4
-            interleave(nc.scalar.copy, w_grp[:, q * WQ : (q + 1) * WQ, :], w_raw[:, q * WQ // (N // 2), :, q * WQ % (N // 2) : q * WQ % (N // 2) + WQ])
-        z_grp = [keep.tile([P, HALF, PACK], BF16, name=f"z_grp{h}", align_bytes=64) for h in range(2)]
-        z_codes = [keep.tile([P, HALF], U32, name=f"z_codes{h}", align_bytes=64) for h in range(2)]
-        z_sc = [keep.tile([P, HALF], U8, name=f"z_sc{h}", align_bytes=64) for h in range(2)]
-        interleave(nc.scalar.copy, z_grp[0][:], zsum[0][:])
-        gather(2, 1)
-        nc.vector.quantize_mx(out=w_codes[:].bitcast(FP8X4), scales=w_sc[:], in_=w_grp[:].rearrange("p m t -> p (m t)"))
-        gather(3, 1)
+        def quantise(codes, scales, grouped):
+            nc.vector.quantize_mx(out=codes[:].bitcast(FP8X4), scales=scales[:], in_=grouped[:].rearrange("p c t -> p (c t)"))
 
-        def finish(h):
-            nc.vector.quantize_mx(out=z_codes[h][:].bitcast(FP8X4), scales=z_sc[h][:], in_=z_grp[h][:].rearrange("p j t -> p (j t)"))
-            for b in range(2):
-                acc = psum.tile([P, 2, HALF], F32, name=f"acc{h}{b}")
-                for u in range(2):
-                    cols = slice((2 * b + u) * P, (2 * b + u + 1) * P)
-                    nc.tensor.matmul_mx(out=acc[:, u, :], lhsT=w_codes[:, cols].bitcast(FP8X4), lhsT_scale=w_sc[:, cols],
-                                        rhs=z_codes[h][:].bitcast(FP8X4), rhs_scale=z_sc[h][:], start=True, stop=True)
-                res = keep.tile([P, 2, HALF], F32, name=f"res{h}{b}")
-                if h == 1 and b == 1:
-                    nc.vector.tensor_copy(res[:], acc[:])
-                else:
-                    nc.scalar.copy(res[:], acc[:])
-                nc.sync.dma_start(out[2 * b * P : (2 * b + 2) * P, h * HALF : (h + 1) * HALF].rearrange("(u p) j -> p u j", p=P), res[:])
+        w_grouped0 = group_w(0, "w_grouped0")
 
-        finish(0)
-        interleave(nc.vector.tensor_copy, z_grp[1][:, 0:176, :], zsum[1][:, :, 0:176])
-        interleave(nc.scalar.copy, z_grp[1][:, 176:HALF, :], zsum[1][:, :, 176:HALF])
-        finish(1)
+        negated, lowest = [], []
+        for t in range(SLOTS):
+            bank = psum.tile([P, S], F32, name=f"scores{t}", tag=f"bank{t}")
+            for cols in halves if t == 0 else [slice(0, S)]:
+                nc.tensor.matmul_mx(
+                    out=bank[:, cols],
+                    lhsT=key_words[t].bitcast(FP8X4),
+                    lhsT_scale=key_scales[:, t * P : (t + 1) * P],
+                    rhs=query_words[:, cols].bitcast(FP8X4),
+                    rhs_scale=query_scales[:, cols],
+                    start=True,
+                    stop=True,
+                )
+            negated.append(keep.tile([P, S], F32, name=f"negated{t}", tag=f"negated{t}", align_bytes=64))
+            lowest.append(keep.tile([P, 1], F32, name=f"lowest{t}"))
+            nc.vector.tensor_scalar(negated[t][:], bank[:], -SCORE_SCALE, None, ALU.mult, ALU.min, accum_out=lowest[t][:])
+
+        starts = [sum(CHUNKS[:h]) for h in range(len(CHUNKS))]
+        first = CHUNKS[0]
+        totals = keep.tile([P, SLOTS], F32, name="totals", tag="picked_scales", align_bytes=64)
+        exps, early, late = [], [], []
+        for t in range(SLOTS):
+            exps.append(keep.tile([P, S], F32, name=f"exps{t}"))
+            late.append(keep.tile([P, S - first], F32, name=f"late{t}"))
+            nc.scalar.activation(exps[t][:], negated[t][:], ACT.Exp, bias=lowest[t][:], scale=-1.0, accum_out=totals[:, t : t + 1])
+            nc.sync.dma_start(late[t][:], exps[t][:, first:S])
+
+        def copy_early(t, tag):
+            early.append(keep.tile([P, first], F32, name=f"early{t}", tag=tag, align_bytes=64))
+            nc.vector.tensor_copy(early[t][:], exps[t][:, 0:first])
+
+        copy_early(0, "early0")
+        w_codes = [
+            keep.tile([P, W_HALF], U32, name="w_codes0", tag="x_word_table", align_bytes=64),
+            keep.tile([P, W_HALF], U32, name="w_codes1", align_bytes=64),
+        ]
+        quantise(w_codes[0], w_scales[0], w_grouped0)
+        inverse = keep.tile([P, SLOTS], F32, name="inverse", tag="inverse", align_bytes=64)
+        factor = keep.tile([P, SLOTS], F32, name="factor")
+        nc.vector.reciprocal(inverse[:], totals[:])
+        copy_early(1, "picked_scales")
+        nc.vector.scalar_tensor_tensor(factor[:], inverse[:], SHARE_SCALE, gn_sb[:], ALU.mult, ALU.mult)
+        copy_early(2, "inverse")
+        copy_early(3, "early3")
+        w_grouped1 = group_w(1, f"negated{SLOTS - 1}")
+
+        def add_neighbours(h, tag):
+            start, width = starts[h], CHUNKS[h]
+            sums = keep.tile([P, SLOTS, width], F32, name=f"sums{h}", tag=tag, align_bytes=64)
+            for t in range(SLOTS):
+                own = early[t][:] if h == 0 else late[t][:, start - first : start - first + width]
+                nc.vector.tensor_tensor(sums[:, t, :], exps[t][:].indirect(entries(nb_sb, start, width)), own, ALU.add)
+            return sums
+
+        def group_on_scalar(h, sums, tag):
+            planes = keep.tile([P, SLOTS, CHUNKS[h]], BF16, name=f"planes{h}", tag="d_word_table", align_bytes=64)
+            for t in range(SLOTS):
+                nc.scalar.activation(planes[:, t, :], sums[:, t, :], ACT.Copy, scale=factor[:, t : t + 1])
+            grouped = keep.tile([P, CHUNKS[h], SLOTS], BF16, name=f"z_grouped{h}", tag=tag, align_bytes=64)
+            nc.scalar.copy(side_by_side(grouped[:]), by_slot(planes[:]))
+            return grouped
+
+        def group_on_vector(h, sums, tag):
+            grouped = keep.tile([P, CHUNKS[h], SLOTS], BF16, name=f"z_grouped{h}", tag=tag, align_bytes=64)
+            spread = factor[:].unsqueeze(1).unsqueeze(3).to_broadcast([P, CHUNKS[h] // RUN, SLOTS, RUN])
+            nc.vector.tensor_tensor(side_by_side(grouped[:]), by_slot(sums[:]), spread, ALU.mult)
+            return grouped
+
+        def multiply(h, grouped, banks):
+            width = CHUNKS[h]
+            z_codes = keep.tile([P, width], U32, name=f"z_codes{h}", align_bytes=64)
+            z_scales = keep.tile([P, width], U8, name=f"z_scales{h}", align_bytes=64)
+            quantise(z_codes, z_scales, grouped)
+            per_bank = N // P // len(banks)
+            for b, (tag, copy, result_tag, queue) in enumerate(banks):
+                acc = psum.tile([P, per_bank, width], F32, name=f"acc{h}_{b}", tag=tag)
+                for u in range(per_bank):
+                    half, first_col = divmod((per_bank * b + u) * P, W_HALF)
+                    cols = slice(first_col, first_col + P)
+                    nc.tensor.matmul_mx(
+                        out=acc[:, u, :],
+                        lhsT=w_codes[half][:, cols].bitcast(FP8X4),
+                        lhsT_scale=w_scales[half][:, cols],
+                        rhs=z_codes[:].bitcast(FP8X4),
+                        rhs_scale=z_scales[:],
+                        start=True,
+                        stop=True,
+                    )
+                result = keep.tile([P, per_bank, width], F32, name=f"result{h}_{b}", tag=result_tag, align_bytes=64)
+                copy(result[:], acc[:])
+                rows = slice(per_bank * b * P, per_bank * (b + 1) * P)
+                queue.dma_start(out[rows, starts[h] : starts[h] + width].rearrange("(u p) j -> p u j", p=P), result[:])
+
+        grouped0 = group_on_scalar(0, add_neighbours(0, "sums0"), "z_grouped0")
+        sums1 = add_neighbours(1, f"early{SLOTS - 1}")
+        quantise(w_codes[1], w_scales[1], w_grouped1)
+        grouped1 = group_on_scalar(1, sums1, "z_grouped1")
+        multiply(0, grouped0, [("bank4", nc.scalar.copy, "d_word_table", nc.sync), ("bank5", nc.scalar.copy, f"early{SLOTS - 1}", nc.sync)])
+        sums2 = add_neighbours(2, "z_grouped0")
+        multiply(1, grouped1, [("bank6", nc.scalar.copy, "result1", nc.sync)])
+        grouped2 = group_on_vector(2, sums2, "z_grouped1")
+        multiply(2, grouped2, [("bank7", nc.scalar.copy, "result2", nc.scalar), ("bank0", nc.vector.tensor_copy, "result3", nc.sync)])

@@ -24,7 +24,6 @@ RUN = 4
 SCORE_SCALE = 0.03125
 SHARE_SCALE = 32.0
 LEAD = 512
-W_HALF = N // 2
 X_HALF = S // 2
 CHUNKS = (256, 128, 128)
 
@@ -54,9 +53,8 @@ def tile_picked_softkeys_none_p_kernel(
         nb_sb = keep.tile([P, S // PER_COLUMN], U16, name="nb_sb")
         d_scale_table = keep.tile([P, G], U8, name="d_scale_table", align_bytes=64)
         x_scale_table = keep.tile([P, T], U8, name="x_scale_table", align_bytes=64)
-        d_word_table = keep.tile([P, G], U32, name="d_word_table", tag="d_word_table", align_bytes=64)
+        d_word_table = keep.tile([P, G], U32, name="d_word_table", align_bytes=64)
         x_word_table = keep.tile([P, T], U32, name="x_word_table", tag="x_word_table", align_bytes=64)
-        key_scales = keep.tile([P, H], U8, name="key_scales", align_bytes=64)
         gn_sb = keep.tile([P, SLOTS], F32, name="gn_sb")
         warm_in = keep.tile([P, 1], F32, name="warm_in")
         warm_out = keep.tile([P, 1], F32, name="warm_out")
@@ -64,7 +62,6 @@ def tile_picked_softkeys_none_p_kernel(
         nc.vector.memset(d_scale_table[:].bitcast(I32), 0)
         nc.vector.memset(x_scale_table[:].bitcast(I32), 0)
         nc.vector.memset(warm_in[:], 0.0)
-        nc.vector.memset(key_scales[:].bitcast(I32), 0)
 
         d_rows = d_words[0].rearrange("p n t -> p (n t)").bitcast(I32)
         nc.sync.dma_start(kidx_sb[:], kidx)
@@ -74,33 +71,26 @@ def tile_picked_softkeys_none_p_kernel(
         nc.sync.dma_start(offs_sb[:], offs)
         for a in range(4):
             nc.scalar.dma_start(x_scale_table[a:P:QUADRANT, :].bitcast(I32), x_scales[0][a : P // BLOCK : 4, :].bitcast(I32))
-        nc.sync.dma_start(x_word_table[:].bitcast(I32), x_words[0].rearrange("p n t -> p (n t)").bitcast(I32))
+        nc.sync.dma_start(x_word_table[:].bitcast(I32), x_words[0].rearrange("p n t -> p (n t)").bitcast(I32), max_dma_last_dim=2048)
         nc.sync.dma_start(nb_sb[:], nb)
         nc.gpsimd.dma_start(gn_sb[:], gn.rearrange("(p t) o -> p (t o)", t=SLOTS))
         nc.scalar.activation(warm_out[:], warm_in[:], ACT.Exp)
 
-        picked_scales = keep.tile([P, H], U8, name="picked_scales", tag="picked_scales", align_bytes=64)
-        dealt_scales = keep.tile([P, H], U8, name="dealt_scales", align_bytes=64)
+        picked_scales = keep.tile([P, H], U8, name="picked_scales", align_bytes=64)
+        key_scales = keep.tile([P, H], U8, name="key_scales", align_bytes=64)
         nc.vector.tensor_copy(picked_scales[:], d_scale_table[:].indirect(kidx_sb[:]))
         nc.vector.tensor_copy(
-            dealt_scales[:].rearrange("p (t m) -> p m t", t=SLOTS), picked_scales[:].rearrange("p (m t) -> p m t", t=SLOTS)
+            key_scales[:].rearrange("p (t m) -> p m t", t=SLOTS), picked_scales[:].rearrange("p (m t) -> p m t", t=SLOTS)
         )
-        for a in range(4):
-            nc.scalar.dma_start(key_scales[a:P:QUADRANT, :].bitcast(I32), dealt_scales[BLOCK * a : P : QUADRANT, :].bitcast(I32))
+        for a in range(1, 4):
+            nc.scalar.dma_start(key_scales[a:P:QUADRANT, :].bitcast(I32), key_scales[BLOCK * a : P : QUADRANT, :].bitcast(I32))
 
-        def load_w(half, tile):
-            cols = slice(half * W_HALF, (half + 1) * W_HALF)
-            nc.sync.dma_start(tile[:], w1[:, cols].rearrange("(p t) m -> p t m", t=SLOTS))
-            return tile
-
-        first_keys = keep.tile([P, P], U32, name="first_keys", align_bytes=64)
+        first_keys = keep.tile([P, P], U32, name="first_keys", tag="first_keys", align_bytes=64)
         query_scales = keep.tile([P, S], U8, name="query_scales", align_bytes=64)
         query_words = keep.tile([P, S], U32, name="query_words", align_bytes=64)
         nc.vector.tensor_copy(query_scales[:], x_scale_table[:].indirect(offs_sb[:]))
-        w_raw = [load_w(0, keep.tile([P, SLOTS, W_HALF], F32, name="w_raw0", tag="picked_scales", align_bytes=64))]
         picked_words = keep.tile([P, H], U32, name="picked_words", align_bytes=64)
         nc.vector.tensor_copy(picked_words[:], d_word_table[:].indirect(kidx_sb[:]))
-        w_raw.append(load_w(1, keep.tile([P, SLOTS, W_HALF], F32, name="w_raw1", tag="d_word_table", align_bytes=64)))
         picked_by_slot = picked_words[:].rearrange("p (m t) -> p m t", t=SLOTS)
         nc.vector.tensor_copy(first_keys[:], picked_by_slot[:, :, 0])
         halves = [slice(0, X_HALF), slice(X_HALF, S)]
@@ -110,17 +100,8 @@ def tile_picked_softkeys_none_p_kernel(
         nc.vector.tensor_copy(other_keys[:].rearrange("p t m -> p m t"), picked_by_slot[:, :, 1:SLOTS])
         key_words = [first_keys[:]] + [other_keys[:, t, :] for t in range(SLOTS - 1)]
 
-        w_scales = [keep.tile([P, W_HALF], U8, name=f"w_scales{h}", align_bytes=64) for h in range(2)]
-
-        def group_w(half, tag):
-            grouped = keep.tile([P, W_HALF, SLOTS], BF16, name=f"w_grouped{half}", tag=tag, align_bytes=64)
-            nc.scalar.copy(side_by_side(grouped[:]), by_slot(w_raw[half][:]))
-            return grouped
-
         def quantise(codes, scales, grouped):
             nc.vector.quantize_mx(out=codes[:].bitcast(FP8X4), scales=scales[:], in_=grouped[:].rearrange("p c t -> p (c t)"))
-
-        w_grouped0 = group_w(0, "w_grouped0")
 
         negated, lowest = [], []
         for t in range(SLOTS):
@@ -135,13 +116,16 @@ def tile_picked_softkeys_none_p_kernel(
                     start=True,
                     stop=True,
                 )
+            if t == 0:
+                w_raw = keep.tile([P, SLOTS, N], F32, name="w_raw", tag="first_keys", align_bytes=64)
+                nc.sync.dma_start(w_raw[:], w1.rearrange("(p t) m -> p t m", t=SLOTS))
             negated.append(keep.tile([P, S], F32, name=f"negated{t}", tag=f"negated{t}", align_bytes=64))
             lowest.append(keep.tile([P, 1], F32, name=f"lowest{t}"))
             nc.vector.tensor_scalar(negated[t][:], bank[:], -SCORE_SCALE, None, ALU.mult, ALU.min, accum_out=lowest[t][:])
 
         starts = [sum(CHUNKS[:h]) for h in range(len(CHUNKS))]
         first = CHUNKS[0]
-        totals = keep.tile([P, SLOTS], F32, name="totals", tag="picked_scales", align_bytes=64)
+        totals = keep.tile([P, SLOTS], F32, name="totals", tag="totals", align_bytes=64)
         exps, early, late = [], [], []
         for t in range(SLOTS):
             exps.append(keep.tile([P, S], F32, name=f"exps{t}"))
@@ -154,19 +138,17 @@ def tile_picked_softkeys_none_p_kernel(
             nc.vector.tensor_copy(early[t][:], exps[t][:, 0:first])
 
         copy_early(0, "early0")
-        w_codes = [
-            keep.tile([P, W_HALF], U32, name="w_codes0", tag="x_word_table", align_bytes=64),
-            keep.tile([P, W_HALF], U32, name="w_codes1", align_bytes=64),
-        ]
-        quantise(w_codes[0], w_scales[0], w_grouped0)
         inverse = keep.tile([P, SLOTS], F32, name="inverse", tag="inverse", align_bytes=64)
         factor = keep.tile([P, SLOTS], F32, name="factor")
         nc.vector.reciprocal(inverse[:], totals[:])
-        copy_early(1, "picked_scales")
+        copy_early(1, "totals")
         nc.vector.scalar_tensor_tensor(factor[:], inverse[:], SHARE_SCALE, gn_sb[:], ALU.mult, ALU.mult)
         copy_early(2, "inverse")
         copy_early(3, "early3")
-        w_grouped1 = group_w(1, f"negated{SLOTS - 1}")
+        w_grouped = keep.tile([P, N, SLOTS], BF16, name="w_grouped", tag=f"negated{SLOTS - 1}", align_bytes=64)
+        w_codes = keep.tile([P, N], U32, name="w_codes", align_bytes=64)
+        w_scales = keep.tile([P, N], U8, name="w_scales", align_bytes=64)
+        nc.scalar.copy(side_by_side(w_grouped[:]), by_slot(w_raw[:]))
 
         def add_neighbours(h, tag):
             start, width = starts[h], CHUNKS[h]
@@ -177,7 +159,7 @@ def tile_picked_softkeys_none_p_kernel(
             return sums
 
         def group_on_scalar(h, sums, tag):
-            planes = keep.tile([P, SLOTS, CHUNKS[h]], BF16, name=f"planes{h}", tag="d_word_table", align_bytes=64)
+            planes = keep.tile([P, SLOTS, CHUNKS[h]], BF16, name=f"planes{h}", tag="first_keys", align_bytes=64)
             for t in range(SLOTS):
                 nc.scalar.activation(planes[:, t, :], sums[:, t, :], ACT.Copy, scale=factor[:, t : t + 1])
             grouped = keep.tile([P, CHUNKS[h], SLOTS], BF16, name=f"z_grouped{h}", tag=tag, align_bytes=64)
@@ -199,12 +181,11 @@ def tile_picked_softkeys_none_p_kernel(
             for b, (tag, copy, result_tag, queue) in enumerate(banks):
                 acc = psum.tile([P, per_bank, width], F32, name=f"acc{h}_{b}", tag=tag)
                 for u in range(per_bank):
-                    half, first_col = divmod((per_bank * b + u) * P, W_HALF)
-                    cols = slice(first_col, first_col + P)
+                    cols = slice((per_bank * b + u) * P, (per_bank * b + u + 1) * P)
                     nc.tensor.matmul_mx(
                         out=acc[:, u, :],
-                        lhsT=w_codes[half][:, cols].bitcast(FP8X4),
-                        lhsT_scale=w_scales[half][:, cols],
+                        lhsT=w_codes[:, cols].bitcast(FP8X4),
+                        lhsT_scale=w_scales[:, cols],
                         rhs=z_codes[:].bitcast(FP8X4),
                         rhs_scale=z_scales[:],
                         start=True,
@@ -217,9 +198,9 @@ def tile_picked_softkeys_none_p_kernel(
 
         grouped0 = group_on_scalar(0, add_neighbours(0, "sums0"), "z_grouped0")
         sums1 = add_neighbours(1, f"early{SLOTS - 1}")
-        quantise(w_codes[1], w_scales[1], w_grouped1)
+        quantise(w_codes, w_scales, w_grouped)
         grouped1 = group_on_scalar(1, sums1, "z_grouped1")
-        multiply(0, grouped0, [("bank4", nc.scalar.copy, "d_word_table", nc.sync), ("bank5", nc.scalar.copy, f"early{SLOTS - 1}", nc.sync)])
+        multiply(0, grouped0, [("bank4", nc.scalar.copy, "first_keys", nc.sync), ("bank5", nc.scalar.copy, f"early{SLOTS - 1}", nc.sync)])
         sums2 = add_neighbours(2, "z_grouped0")
         multiply(1, grouped1, [("bank6", nc.scalar.copy, "result1", nc.sync)])
         grouped2 = group_on_vector(2, sums2, "z_grouped1")

@@ -23,8 +23,11 @@ BLOCK = 8
 RUN = 4
 SCORE_SCALE = 0.03125
 SHARE_SCALE = 32.0
+SCALE_ROWS = 4
 LEAD = 512
+X_PIECE_BYTES = 2048
 X_HALF = S // 2
+W_HALF = N // 2
 CHUNKS = (256, 128, 128)
 
 
@@ -56,12 +59,9 @@ def tile_picked_softkeys_none_p_kernel(
         d_word_table = keep.tile([P, G], U32, name="d_word_table", align_bytes=64)
         x_word_table = keep.tile([P, T], U32, name="x_word_table", tag="x_word_table", align_bytes=64)
         gn_sb = keep.tile([P, SLOTS], F32, name="gn_sb")
-        warm_in = keep.tile([P, 1], F32, name="warm_in")
-        warm_out = keep.tile([P, 1], F32, name="warm_out")
 
         nc.vector.memset(d_scale_table[:].bitcast(I32), 0)
         nc.vector.memset(x_scale_table[:].bitcast(I32), 0)
-        nc.vector.memset(warm_in[:], 0.0)
 
         d_rows = d_words[0].rearrange("p n t -> p (n t)").bitcast(I32)
         nc.sync.dma_start(kidx_sb[:], kidx)
@@ -69,21 +69,25 @@ def tile_picked_softkeys_none_p_kernel(
         nc.sync.dma_start(d_scale_table[0:P:BLOCK, :].bitcast(I32), d_scales[0].bitcast(I32))
         nc.sync.dma_start(d_word_table[:, LEAD:G].bitcast(I32), d_rows[:, LEAD:G])
         nc.sync.dma_start(offs_sb[:], offs)
-        for a in range(4):
-            nc.scalar.dma_start(x_scale_table[a:P:QUADRANT, :].bitcast(I32), x_scales[0][a : P // BLOCK : 4, :].bitcast(I32))
-        nc.sync.dma_start(x_word_table[:].bitcast(I32), x_words[0].rearrange("p n t -> p (n t)").bitcast(I32), max_dma_last_dim=2048)
+        for a in range(SCALE_ROWS):
+            rows = x_scales[0][a : P // BLOCK : SCALE_ROWS, :]
+            nc.scalar.dma_start(x_scale_table[a:P:QUADRANT, :].bitcast(I32), rows.bitcast(I32))
+        x_rows = x_words[0].rearrange("p n t -> p (n t)").bitcast(I32)
+        nc.sync.dma_start(x_word_table[:].bitcast(I32), x_rows, max_dma_last_dim=X_PIECE_BYTES)
         nc.sync.dma_start(nb_sb[:], nb)
         nc.gpsimd.dma_start(gn_sb[:], gn.rearrange("(p t) o -> p (t o)", t=SLOTS))
-        nc.scalar.activation(warm_out[:], warm_in[:], ACT.Exp)
 
-        picked_scales = keep.tile([P, H], U8, name="picked_scales", align_bytes=64)
+        picked_scales = keep.tile([P, H], U8, name="picked_scales", tag="picked_scales", align_bytes=64)
         key_scales = keep.tile([P, H], U8, name="key_scales", align_bytes=64)
         nc.vector.tensor_copy(picked_scales[:], d_scale_table[:].indirect(kidx_sb[:]))
         nc.vector.tensor_copy(
             key_scales[:].rearrange("p (t m) -> p m t", t=SLOTS), picked_scales[:].rearrange("p (m t) -> p m t", t=SLOTS)
         )
-        for a in range(1, 4):
+        for a in range(1, SCALE_ROWS):
             nc.scalar.dma_start(key_scales[a:P:QUADRANT, :].bitcast(I32), key_scales[BLOCK * a : P : QUADRANT, :].bitcast(I32))
+
+        weight = keep.tile([P, SLOTS], F32, name="weight", tag="picked_scales", align_bytes=64)
+        nc.scalar.activation(weight[:], gn_sb[:], ACT.Copy, scale=SHARE_SCALE)
 
         first_keys = keep.tile([P, P], U32, name="first_keys", tag="first_keys", align_bytes=64)
         query_scales = keep.tile([P, S], U8, name="query_scales", align_bytes=64)
@@ -117,8 +121,10 @@ def tile_picked_softkeys_none_p_kernel(
                     stop=True,
                 )
             if t == 0:
-                w_raw = keep.tile([P, SLOTS, N], F32, name="w_raw", tag="first_keys", align_bytes=64)
-                nc.sync.dma_start(w_raw[:], w1.rearrange("(p t) m -> p t m", t=SLOTS))
+                w_raw = keep.tile([P, 2, SLOTS, W_HALF], F32, name="w_raw", tag="first_keys", align_bytes=64)
+                for half in range(2):
+                    w_cols = w1[:, half * W_HALF : (half + 1) * W_HALF]
+                    nc.sync.dma_start(w_raw[:, half], w_cols.rearrange("(p t) m -> p t m", t=SLOTS))
             negated.append(keep.tile([P, S], F32, name=f"negated{t}", tag=f"negated{t}", align_bytes=64))
             lowest.append(keep.tile([P, 1], F32, name=f"lowest{t}"))
             nc.vector.tensor_scalar(negated[t][:], bank[:], -SCORE_SCALE, None, ALU.mult, ALU.min, accum_out=lowest[t][:])
@@ -142,13 +148,15 @@ def tile_picked_softkeys_none_p_kernel(
         factor = keep.tile([P, SLOTS], F32, name="factor")
         nc.vector.reciprocal(inverse[:], totals[:])
         copy_early(1, "totals")
-        nc.vector.scalar_tensor_tensor(factor[:], inverse[:], SHARE_SCALE, gn_sb[:], ALU.mult, ALU.mult)
+        nc.vector.tensor_tensor(factor[:], inverse[:], weight[:], ALU.mult)
         copy_early(2, "inverse")
         copy_early(3, "early3")
-        w_grouped = keep.tile([P, N, SLOTS], BF16, name="w_grouped", tag=f"negated{SLOTS - 1}", align_bytes=64)
+
+        w_grouped = keep.tile([P, N, SLOTS], BF16, name="w_grouped", tag="negated3", align_bytes=64)
         w_codes = keep.tile([P, N], U32, name="w_codes", align_bytes=64)
         w_scales = keep.tile([P, N], U8, name="w_scales", align_bytes=64)
-        nc.scalar.copy(side_by_side(w_grouped[:]), by_slot(w_raw[:]))
+        for half in range(2):
+            nc.scalar.copy(side_by_side(w_grouped[:, half * W_HALF : (half + 1) * W_HALF, :]), by_slot(w_raw[:, half]))
 
         def add_neighbours(h, tag):
             start, width = starts[h], CHUNKS[h]
@@ -178,14 +186,14 @@ def tile_picked_softkeys_none_p_kernel(
             z_scales = keep.tile([P, width], U8, name=f"z_scales{h}", align_bytes=64)
             quantise(z_codes, z_scales, grouped)
             per_bank = N // P // len(banks)
-            for b, (tag, copy, result_tag, queue) in enumerate(banks):
-                acc = psum.tile([P, per_bank, width], F32, name=f"acc{h}_{b}", tag=tag)
+            for b, (bank_tag, copy, result_tag, queue) in enumerate(banks):
+                acc = psum.tile([P, per_bank, width], F32, name=f"acc{h}_{b}", tag=bank_tag)
                 for u in range(per_bank):
-                    cols = slice((per_bank * b + u) * P, (per_bank * b + u + 1) * P)
+                    out_rows = slice((per_bank * b + u) * P, (per_bank * b + u + 1) * P)
                     nc.tensor.matmul_mx(
                         out=acc[:, u, :],
-                        lhsT=w_codes[:, cols].bitcast(FP8X4),
-                        lhsT_scale=w_scales[:, cols],
+                        lhsT=w_codes[:, out_rows].bitcast(FP8X4),
+                        lhsT_scale=w_scales[:, out_rows],
                         rhs=z_codes[:].bitcast(FP8X4),
                         rhs_scale=z_scales[:],
                         start=True,
@@ -193,14 +201,14 @@ def tile_picked_softkeys_none_p_kernel(
                     )
                 result = keep.tile([P, per_bank, width], F32, name=f"result{h}_{b}", tag=result_tag, align_bytes=64)
                 copy(result[:], acc[:])
-                rows = slice(per_bank * b * P, per_bank * (b + 1) * P)
-                queue.dma_start(out[rows, starts[h] : starts[h] + width].rearrange("(u p) j -> p u j", p=P), result[:])
+                bank_rows = slice(per_bank * b * P, per_bank * (b + 1) * P)
+                queue.dma_start(out[bank_rows, starts[h] : starts[h] + width].rearrange("(u p) j -> p u j", p=P), result[:])
 
         grouped0 = group_on_scalar(0, add_neighbours(0, "sums0"), "z_grouped0")
-        sums1 = add_neighbours(1, f"early{SLOTS - 1}")
+        sums1 = add_neighbours(1, "early3")
         quantise(w_codes, w_scales, w_grouped)
         grouped1 = group_on_scalar(1, sums1, "z_grouped1")
-        multiply(0, grouped0, [("bank4", nc.scalar.copy, "first_keys", nc.sync), ("bank5", nc.scalar.copy, f"early{SLOTS - 1}", nc.sync)])
+        multiply(0, grouped0, [("bank4", nc.scalar.copy, "first_keys", nc.sync), ("bank5", nc.scalar.copy, "early3", nc.sync)])
         sums2 = add_neighbours(2, "z_grouped0")
         multiply(1, grouped1, [("bank6", nc.scalar.copy, "result1", nc.sync)])
         grouped2 = group_on_vector(2, sums2, "z_grouped1")

@@ -28,7 +28,8 @@ LEAD = 512
 X_PIECE_BYTES = 2048
 X_HALF = S // 2
 W_HALF = N // 2
-CHUNKS = (256, 128, 128)
+HALF = S // 2
+QUARTER = S // 4
 
 
 def side_by_side(grouped):
@@ -56,7 +57,7 @@ def tile_picked_softkeys_none_p_kernel(
         nb_sb = keep.tile([P, S // PER_COLUMN], U16, name="nb_sb")
         d_scale_table = keep.tile([P, G], U8, name="d_scale_table", align_bytes=64)
         x_scale_table = keep.tile([P, T], U8, name="x_scale_table", align_bytes=64)
-        d_word_table = keep.tile([P, G], U32, name="d_word_table", align_bytes=64)
+        d_word_table = keep.tile([P, G], U32, name="d_word_table", tag="d_word_table", align_bytes=64)
         x_word_table = keep.tile([P, T], U32, name="x_word_table", tag="x_word_table", align_bytes=64)
         gn_sb = keep.tile([P, SLOTS], F32, name="gn_sb")
 
@@ -86,8 +87,12 @@ def tile_picked_softkeys_none_p_kernel(
         for a in range(1, SCALE_ROWS):
             nc.scalar.dma_start(key_scales[a:P:QUADRANT, :].bitcast(I32), key_scales[BLOCK * a : P : QUADRANT, :].bitcast(I32))
 
-        weight = keep.tile([P, SLOTS], F32, name="weight", tag="picked_scales", align_bytes=64)
-        nc.scalar.activation(weight[:], gn_sb[:], ACT.Copy, scale=SHARE_SCALE)
+        w_raw = keep.tile([P, 2 * SLOTS * W_HALF], F32, name="w_raw", tag="picked_scales", align_bytes=64)
+        w_halves = [w_raw[:, half * SLOTS * W_HALF : (half + 1) * SLOTS * W_HALF].rearrange("p (t m) -> p t m", t=SLOTS) for half in range(2)]
+        for half in range(2):
+            w_cols = w1[:, half * W_HALF : (half + 1) * W_HALF]
+            nc.scalar.dma_start(w_halves[half], w_cols.rearrange("(p t) m -> p t m", t=SLOTS))
+        weight = keep.tile([P, SLOTS], F32, name="weight", tag="d_word_table", align_bytes=64)
 
         first_keys = keep.tile([P, P], U32, name="first_keys", tag="first_keys", align_bytes=64)
         query_scales = keep.tile([P, S], U8, name="query_scales", align_bytes=64)
@@ -95,6 +100,10 @@ def tile_picked_softkeys_none_p_kernel(
         nc.vector.tensor_copy(query_scales[:], x_scale_table[:].indirect(offs_sb[:]))
         picked_words = keep.tile([P, H], U32, name="picked_words", align_bytes=64)
         nc.vector.tensor_copy(picked_words[:], d_word_table[:].indirect(kidx_sb[:]))
+        nc.scalar.activation(weight[:], gn_sb[:], ACT.Copy, scale=SHARE_SCALE)
+        w_grouped = [keep.tile([P, W_HALF, SLOTS], BF16, name=f"w_grouped{half}", tag=f"w_grouped{half}", align_bytes=64) for half in range(2)]
+        nc.scalar.copy(side_by_side(w_grouped[0][:]), by_slot(w_halves[0]))
+        nc.gpsimd.tensor_scalar(side_by_side(w_grouped[1][:]), by_slot(w_halves[1]), 1.0, 0.0, ALU.mult, ALU.add)
         picked_by_slot = picked_words[:].rearrange("p (m t) -> p m t", t=SLOTS)
         nc.vector.tensor_copy(first_keys[:], picked_by_slot[:, :, 0])
         halves = [slice(0, X_HALF), slice(X_HALF, S)]
@@ -120,96 +129,89 @@ def tile_picked_softkeys_none_p_kernel(
                     start=True,
                     stop=True,
                 )
-            if t == 0:
-                w_raw = keep.tile([P, 2, SLOTS, W_HALF], F32, name="w_raw", tag="first_keys", align_bytes=64)
-                for half in range(2):
-                    w_cols = w1[:, half * W_HALF : (half + 1) * W_HALF]
-                    nc.sync.dma_start(w_raw[:, half], w_cols.rearrange("(p t) m -> p t m", t=SLOTS))
             negated.append(keep.tile([P, S], F32, name=f"negated{t}", tag=f"negated{t}", align_bytes=64))
             lowest.append(keep.tile([P, 1], F32, name=f"lowest{t}"))
             nc.vector.tensor_scalar(negated[t][:], bank[:], -SCORE_SCALE, None, ALU.mult, ALU.min, accum_out=lowest[t][:])
 
-        starts = [sum(CHUNKS[:h]) for h in range(len(CHUNKS))]
-        first = CHUNKS[0]
-        totals = keep.tile([P, SLOTS], F32, name="totals", tag="totals", align_bytes=64)
-        exps, early, late = [], [], []
+        last = SLOTS - 1
+        totals = keep.tile([P, SLOTS], F32, name="totals", align_bytes=64)
+        exps, shares = [], []
         for t in range(SLOTS):
-            exps.append(keep.tile([P, S], F32, name=f"exps{t}"))
-            late.append(keep.tile([P, S - first], F32, name=f"late{t}"))
+            exps.append(keep.tile([P, S], F32, name=f"exps{t}", tag=f"exps{t}", align_bytes=64))
+            shares.append(keep.tile([P, S], F32, name=f"shares{t}", align_bytes=64))
             nc.scalar.activation(exps[t][:], negated[t][:], ACT.Exp, bias=lowest[t][:], scale=-1.0, accum_out=totals[:, t : t + 1])
-            nc.sync.dma_start(late[t][:], exps[t][:, first:S])
 
-        def copy_early(t, tag):
-            early.append(keep.tile([P, first], F32, name=f"early{t}", tag=tag, align_bytes=64))
-            nc.vector.tensor_copy(early[t][:], exps[t][:, 0:first])
+        w_codes, w_scales = [], []
 
-        copy_early(0, "early0")
-        inverse = keep.tile([P, SLOTS], F32, name="inverse", tag="inverse", align_bytes=64)
-        factor = keep.tile([P, SLOTS], F32, name="factor")
-        nc.vector.reciprocal(inverse[:], totals[:])
-        copy_early(1, "totals")
-        nc.vector.tensor_tensor(factor[:], inverse[:], weight[:], ALU.mult)
-        copy_early(2, "inverse")
-        copy_early(3, "early3")
+        def quantise_w(half, tag):
+            w_codes.append(keep.tile([P, W_HALF], U32, name=f"w_codes{half}", tag=tag, align_bytes=64))
+            w_scales.append(keep.tile([P, W_HALF], U8, name=f"w_scales{half}", align_bytes=64))
+            quantise(w_codes[half], w_scales[half], w_grouped[half])
 
-        w_grouped = keep.tile([P, N, SLOTS], BF16, name="w_grouped", tag="negated3", align_bytes=64)
-        w_codes = keep.tile([P, N], U32, name="w_codes", align_bytes=64)
-        w_scales = keep.tile([P, N], U8, name="w_scales", align_bytes=64)
-        for half in range(2):
-            nc.scalar.copy(side_by_side(w_grouped[:, half * W_HALF : (half + 1) * W_HALF, :]), by_slot(w_raw[:, half]))
+        inverse = keep.tile([P, SLOTS], F32, name="inverse", align_bytes=64)
+        own = keep.tile([P, SLOTS * S], F32, name="own", align_bytes=64)
+        own_slots = own[:].rearrange("p (t j) -> p t j", t=SLOTS)
 
-        def add_neighbours(h, tag):
-            start, width = starts[h], CHUNKS[h]
-            sums = keep.tile([P, SLOTS, width], F32, name=f"sums{h}", tag=tag, align_bytes=64)
-            for t in range(SLOTS):
-                own = early[t][:] if h == 0 else late[t][:, start - first : start - first + width]
-                nc.vector.tensor_tensor(sums[:, t, :], exps[t][:].indirect(entries(nb_sb, start, width)), own, ALU.add)
-            return sums
+        def scale(target, t):
+            nc.vector.tensor_scalar(target, exps[t][:], inverse[:, t : t + 1], weight[:, t : t + 1], ALU.mult, ALU.mult)
 
-        def group_on_scalar(h, sums, tag):
-            planes = keep.tile([P, SLOTS, CHUNKS[h]], BF16, name=f"planes{h}", tag="first_keys", align_bytes=64)
-            for t in range(SLOTS):
-                nc.scalar.activation(planes[:, t, :], sums[:, t, :], ACT.Copy, scale=factor[:, t : t + 1])
-            grouped = keep.tile([P, CHUNKS[h], SLOTS], BF16, name=f"z_grouped{h}", tag=tag, align_bytes=64)
-            nc.scalar.copy(side_by_side(grouped[:]), by_slot(planes[:]))
+        quantise_w(0, "x_word_table")
+        nc.vector.reciprocal(inverse[:, 0:last], totals[:, 0:last])
+        scale(shares[0][:], 0)
+        scale(shares[1][:], 1)
+        nc.vector.reciprocal(inverse[:, last:SLOTS], totals[:, last:SLOTS])
+        scale(shares[2][:], 2)
+        scale(shares[3][:], 3)
+        for t in (3, 0, 1, 2):
+            scale(own_slots[:, t, :], t)
+        quantise_w(1, "exps2")
+
+        def fetch(fetched, t, start, on_vector):
+            window = shares[t][:].indirect(entries(nb_sb, start, HALF))
+            if on_vector:
+                nc.vector.tensor_copy(fetched[:, t, :], window)
+            else:
+                nc.scalar.activation(fetched[:, t, :], window, ACT.Copy)
+
+        def group(name, fetched, start, width, tag):
+            grouped = keep.tile([P, width, SLOTS], BF16, name=name, tag=tag, align_bytes=64)
+            nc.vector.tensor_tensor(side_by_side(grouped[:]), by_slot(fetched), by_slot(own_slots[:, :, start : start + width]), ALU.add)
             return grouped
 
-        def group_on_vector(h, sums, tag):
-            grouped = keep.tile([P, CHUNKS[h], SLOTS], BF16, name=f"z_grouped{h}", tag=tag, align_bytes=64)
-            spread = factor[:].unsqueeze(1).unsqueeze(3).to_broadcast([P, CHUNKS[h] // RUN, SLOTS, RUN])
-            nc.vector.tensor_tensor(side_by_side(grouped[:]), by_slot(sums[:]), spread, ALU.mult)
-            return grouped
-
-        def multiply(h, grouped, banks):
-            width = CHUNKS[h]
-            z_codes = keep.tile([P, width], U32, name=f"z_codes{h}", align_bytes=64)
-            z_scales = keep.tile([P, width], U8, name=f"z_scales{h}", align_bytes=64)
+        def multiply(grouped, start, width, banks):
+            z_codes = keep.tile([P, width], U32, name=f"z_codes{start}", align_bytes=64)
+            z_scales = keep.tile([P, width], U8, name=f"z_scales{start}", align_bytes=64)
             quantise(z_codes, z_scales, grouped)
             per_bank = N // P // len(banks)
-            for b, (bank_tag, copy, result_tag, queue) in enumerate(banks):
-                acc = psum.tile([P, per_bank, width], F32, name=f"acc{h}_{b}", tag=bank_tag)
+            for b, (bank_tag, copy, queue) in enumerate(banks):
+                acc = psum.tile([P, per_bank, width], F32, name=f"acc{start}_{b}", tag=bank_tag)
                 for u in range(per_bank):
-                    out_rows = slice((per_bank * b + u) * P, (per_bank * b + u + 1) * P)
+                    half, block = divmod(per_bank * b + u, W_HALF // P)
+                    out_rows = slice(block * P, (block + 1) * P)
                     nc.tensor.matmul_mx(
                         out=acc[:, u, :],
-                        lhsT=w_codes[:, out_rows].bitcast(FP8X4),
-                        lhsT_scale=w_scales[:, out_rows],
+                        lhsT=w_codes[half][:, out_rows].bitcast(FP8X4),
+                        lhsT_scale=w_scales[half][:, out_rows],
                         rhs=z_codes[:].bitcast(FP8X4),
                         rhs_scale=z_scales[:],
                         start=True,
                         stop=True,
                     )
-                result = keep.tile([P, per_bank, width], F32, name=f"result{h}_{b}", tag=result_tag, align_bytes=64)
+                result = keep.tile([P, per_bank, width], F32, name=f"result{start}_{b}", align_bytes=64)
                 copy(result[:], acc[:])
                 bank_rows = slice(per_bank * b * P, per_bank * (b + 1) * P)
-                queue.dma_start(out[bank_rows, starts[h] : starts[h] + width].rearrange("(u p) j -> p u j", p=P), result[:])
+                queue.dma_start(out[bank_rows, start : start + width].rearrange("(u p) j -> p u j", p=P), result[:])
 
-        grouped0 = group_on_scalar(0, add_neighbours(0, "sums0"), "z_grouped0")
-        sums1 = add_neighbours(1, "early3")
-        quantise(w_codes, w_scales, w_grouped)
-        grouped1 = group_on_scalar(1, sums1, "z_grouped1")
-        multiply(0, grouped0, [("bank4", nc.scalar.copy, "first_keys", nc.sync), ("bank5", nc.scalar.copy, "early3", nc.sync)])
-        sums2 = add_neighbours(2, "z_grouped0")
-        multiply(1, grouped1, [("bank6", nc.scalar.copy, "result1", nc.sync)])
-        grouped2 = group_on_vector(2, sums2, "z_grouped1")
-        multiply(2, grouped2, [("bank7", nc.scalar.copy, "result2", nc.scalar), ("bank0", nc.vector.tensor_copy, "result3", nc.sync)])
+        fetched0 = keep.tile([P, SLOTS, HALF], F32, name="fetched0", tag="fetched0", align_bytes=64)
+        fetched1 = keep.tile([P, SLOTS, HALF], F32, name="fetched1", tag="exps3", align_bytes=64)
+        for t in range(SLOTS):
+            fetch(fetched0, t, 0, False)
+        for t in range(last):
+            fetch(fetched1, t, HALF, False)
+        grouped0 = group("grouped0", fetched0[:], 0, HALF, "grouped0")
+        fetch(fetched1, last, HALF, True)
+        multiply(grouped0, 0, HALF, [("bank4", nc.scalar.copy, nc.sync), ("bank5", nc.scalar.copy, nc.sync)])
+        grouped1 = group("grouped1", fetched1[:, :, 0:QUARTER], HALF, QUARTER, "grouped0")
+        grouped2 = group("grouped2", fetched1[:, :, QUARTER:HALF], HALF + QUARTER, QUARTER, "fetched0")
+        multiply(grouped1, HALF, QUARTER, [("bank6", nc.scalar.copy, nc.sync)])
+        multiply(grouped2, HALF + QUARTER, QUARTER, [("bank7", nc.vector.tensor_copy, nc.scalar)])

@@ -114,7 +114,7 @@ def tile_picked_softkeys_none_p_kernel(
         key_words = [first_keys[:]] + [other_keys[:, t, :] for t in range(SLOTS - 1)]
 
         def quantise(codes, scales, grouped):
-            nc.vector.quantize_mx(out=codes[:].bitcast(FP8X4), scales=scales[:], in_=grouped[:].rearrange("p c t -> p (c t)"))
+            nc.vector.quantize_mx(out=codes[:].bitcast(FP8X4), scales=scales[:], in_=grouped.rearrange("p c t -> p (c t)"))
 
         negated, lowest = [], []
         for t in range(SLOTS):
@@ -146,14 +146,16 @@ def tile_picked_softkeys_none_p_kernel(
         def quantise_w(half, tag):
             w_codes.append(keep.tile([P, W_HALF], U32, name=f"w_codes{half}", tag=tag, align_bytes=64))
             w_scales.append(keep.tile([P, W_HALF], U8, name=f"w_scales{half}", align_bytes=64))
-            quantise(w_codes[half], w_scales[half], w_grouped[half])
+            quantise(w_codes[half], w_scales[half], w_grouped[half][:])
 
         inverse = keep.tile([P, SLOTS], F32, name="inverse", align_bytes=64)
-        own = keep.tile([P, SLOTS * S], F32, name="own", align_bytes=64)
+        own = keep.tile([P, SLOTS * HALF], F32, name="own", align_bytes=64)
         own_slots = own[:].rearrange("p (t j) -> p t j", t=SLOTS)
+        own_late = keep.tile([P, SLOTS * HALF], F32, name="own_late", align_bytes=64)
+        late_slots = own_late[:].rearrange("p (t j) -> p t j", t=SLOTS)
 
-        def scale(target, t):
-            nc.vector.tensor_scalar(target, exps[t][:], inverse[:, t : t + 1], weight[:, t : t + 1], ALU.mult, ALU.mult)
+        def scale(target, t, width=S):
+            nc.vector.tensor_scalar(target, exps[t][:, 0:width], inverse[:, t : t + 1], weight[:, t : t + 1], ALU.mult, ALU.mult)
 
         quantise_w(0, "x_word_table")
         nc.vector.reciprocal(inverse[:, 0:last], totals[:, 0:last])
@@ -163,15 +165,17 @@ def tile_picked_softkeys_none_p_kernel(
         scale(shares[2][:], 2)
         scale(shares[3][:], 3)
         for t in (3, 0, 1, 2):
-            scale(own_slots[:, t, :], t)
+            scale(own_slots[:, t, :], t, HALF)
         quantise_w(1, "exps2")
+        for t in range(SLOTS):
+            nc.sync.dma_start(late_slots[:, t, :], shares[t][:, HALF:S])
 
-        def fetch(fetched, t, start, on_vector):
-            window = shares[t][:].indirect(entries(nb_sb, start, HALF))
+        def fetch(target, t, start, width, on_vector):
+            window = shares[t][:].indirect(entries(nb_sb, start, width))
             if on_vector:
-                nc.vector.tensor_copy(fetched[:, t, :], window)
+                nc.vector.tensor_copy(target, window)
             else:
-                nc.scalar.activation(fetched[:, t, :], window, ACT.Copy)
+                nc.scalar.activation(target, window, ACT.Copy)
 
         def group(name, fetched, start, width, tag):
             grouped = keep.tile([P, width, SLOTS], BF16, name=name, tag=tag, align_bytes=64)
@@ -205,13 +209,16 @@ def tile_picked_softkeys_none_p_kernel(
         fetched0 = keep.tile([P, SLOTS, HALF], F32, name="fetched0", tag="fetched0", align_bytes=64)
         fetched1 = keep.tile([P, SLOTS, HALF], F32, name="fetched1", tag="exps3", align_bytes=64)
         for t in range(SLOTS):
-            fetch(fetched0, t, 0, False)
+            fetch(fetched0[:, t, :], t, 0, HALF, t == last)
         for t in range(last):
-            fetch(fetched1, t, HALF, False)
+            fetch(fetched1[:, t, :], t, HALF, HALF, False)
+        fetch(fetched1[:, last, QUARTER:HALF], last, HALF + QUARTER, QUARTER, False)
         grouped0 = group("grouped0", fetched0[:], 0, HALF, "grouped0")
-        fetch(fetched1, last, HALF, True)
-        multiply(grouped0, 0, HALF, [("bank4", nc.scalar.copy, nc.sync), ("bank5", nc.scalar.copy, nc.sync)])
-        grouped1 = group("grouped1", fetched1[:, :, 0:QUARTER], HALF, QUARTER, "grouped0")
-        grouped2 = group("grouped2", fetched1[:, :, QUARTER:HALF], HALF + QUARTER, QUARTER, "fetched0")
+        fetch(fetched1[:, last, 0:QUARTER], last, HALF, QUARTER, True)
+        multiply(grouped0[:], 0, HALF, [("bank4", nc.scalar.copy, nc.sync), ("bank5", nc.scalar.copy, nc.sync)])
+        late = keep.tile([P, HALF, SLOTS], BF16, name="late", tag="grouped0", align_bytes=64)
+        grouped1, grouped2 = late[:, 0:QUARTER, :], late[:, QUARTER:HALF, :]
+        for part, start in ((grouped1, 0), (grouped2, QUARTER)):
+            nc.vector.tensor_tensor(side_by_side(part), by_slot(fetched1[:, :, start : start + QUARTER]), by_slot(late_slots[:, :, start : start + QUARTER]), ALU.add)
         multiply(grouped1, HALF, QUARTER, [("bank6", nc.scalar.copy, nc.sync)])
-        multiply(grouped2, HALF + QUARTER, QUARTER, [("bank7", nc.vector.tensor_copy, nc.scalar)])
+        multiply(grouped2, HALF + QUARTER, QUARTER, [("bank7", nc.vector.tensor_copy, nc.sync), ("bank0", nc.scalar.copy, nc.scalar)])

@@ -32,12 +32,12 @@ HALF = S // 2
 QUARTER = S // 4
 
 
-def side_by_side(grouped):
-    return grouped.rearrange("p (c i) t -> p c t i", i=RUN)
+def side_by_side(grouped, run=RUN):
+    return grouped.rearrange("p (c i) t -> p c t i", i=run)
 
 
-def by_slot(planes):
-    return planes.rearrange("p t (c i) -> p c t i", i=RUN)
+def by_slot(planes, run=RUN):
+    return planes.rearrange("p t (c i) -> p c t i", i=run)
 
 
 def entries(offsets, start, count):
@@ -179,7 +179,7 @@ def tile_picked_softkeys_none_p_kernel(
 
         def group(name, fetched, start, width, tag):
             grouped = keep.tile([P, width, SLOTS], BF16, name=name, tag=tag, align_bytes=64)
-            nc.vector.tensor_tensor(side_by_side(grouped[:]), by_slot(fetched), by_slot(own_slots[:, :, start : start + width]), ALU.add)
+            nc.vector.tensor_tensor(side_by_side(grouped[:], 2), by_slot(fetched, 2), by_slot(own_slots[:, :, start : start + width], 2), ALU.add)
             return grouped
 
         def multiply(grouped, start, width, banks):
@@ -212,13 +212,12 @@ def tile_picked_softkeys_none_p_kernel(
             fetch(fetched0[:, t, :], t, 0, HALF, t == last)
         for t in range(last):
             fetch(fetched1[:, t, :], t, HALF, HALF, False)
-        fetch(fetched1[:, last, QUARTER:HALF], last, HALF + QUARTER, QUARTER, False)
+        fetch(fetched1[:, last, :], last, HALF, HALF, False)
         grouped0 = group("grouped0", fetched0[:], 0, HALF, "grouped0")
-        fetch(fetched1[:, last, 0:QUARTER], last, HALF, QUARTER, True)
         multiply(grouped0[:], 0, HALF, [("bank4", nc.scalar.copy, nc.sync), ("bank5", nc.scalar.copy, nc.sync)])
         late = keep.tile([P, HALF, SLOTS], BF16, name="late", tag="grouped0", align_bytes=64)
         grouped1, grouped2 = late[:, 0:QUARTER, :], late[:, QUARTER:HALF, :]
         for part, start in ((grouped1, 0), (grouped2, QUARTER)):
-            nc.vector.tensor_tensor(side_by_side(part), by_slot(fetched1[:, :, start : start + QUARTER]), by_slot(late_slots[:, :, start : start + QUARTER]), ALU.add)
+            nc.vector.tensor_tensor(side_by_side(part, 2), by_slot(fetched1[:, :, start : start + QUARTER], 2), by_slot(late_slots[:, :, start : start + QUARTER], 2), ALU.add)
         multiply(grouped1, HALF, QUARTER, [("bank6", nc.scalar.copy, nc.sync)])
         multiply(grouped2, HALF + QUARTER, QUARTER, [("bank7", nc.vector.tensor_copy, nc.sync), ("bank0", nc.scalar.copy, nc.scalar)])

@@ -101,9 +101,12 @@ def tile_picked_softkeys_none_p_kernel(
         picked_words = keep.tile([P, H], U32, name="picked_words", align_bytes=64)
         nc.vector.tensor_copy(picked_words[:], d_word_table[:].indirect(kidx_sb[:]))
         nc.scalar.activation(weight[:], gn_sb[:], ACT.Copy, scale=SHARE_SCALE)
-        w_grouped = [keep.tile([P, W_HALF, SLOTS], BF16, name=f"w_grouped{half}", tag=f"w_grouped{half}", align_bytes=64) for half in range(2)]
-        nc.scalar.copy(side_by_side(w_grouped[0][:]), by_slot(w_halves[0]))
-        nc.gpsimd.tensor_scalar(side_by_side(w_grouped[1][:]), by_slot(w_halves[1]), 1.0, 0.0, ALU.mult, ALU.add)
+        w_grouped = [keep.tile([P, P, SLOTS], BF16, name=f"w_grouped{u}", tag=f"w_grouped{u}", align_bytes=64) for u in range(N // P)]
+        for u in range(2):
+            nc.scalar.copy(side_by_side(w_grouped[u][:]), by_slot(w_halves[0][:, :, u * P : (u + 1) * P]))
+        for u in range(2):
+            columns = w_halves[1][:, :, u * P : (u + 1) * P].rearrange("p t c -> p c t")
+            nc.gpsimd.tensor_scalar(w_grouped[2 + u][:], columns, 1.0, 0.0, ALU.mult, ALU.add)
         picked_by_slot = picked_words[:].rearrange("p (m t) -> p m t", t=SLOTS)
         nc.vector.tensor_copy(first_keys[:], picked_by_slot[:, :, 0])
         halves = [slice(0, X_HALF), slice(X_HALF, S)]
@@ -144,8 +147,8 @@ def tile_picked_softkeys_none_p_kernel(
         w_codes, w_scales = [], []
 
         def quantise_w(half, tag):
-            w_codes.append(keep.tile([P, W_HALF], U32, name=f"w_codes{half}", tag=tag, align_bytes=64))
-            w_scales.append(keep.tile([P, W_HALF], U8, name=f"w_scales{half}", align_bytes=64))
+            w_codes.append(keep.tile([P, P], U32, name=f"w_codes{half}", tag=tag, align_bytes=64))
+            w_scales.append(keep.tile([P, P], U8, name=f"w_scales{half}", align_bytes=64))
             quantise(w_codes[half], w_scales[half], w_grouped[half][:])
 
         inverse = keep.tile([P, SLOTS], F32, name="inverse", align_bytes=64)
@@ -159,6 +162,7 @@ def tile_picked_softkeys_none_p_kernel(
 
         quantise_w(0, "x_word_table")
         nc.vector.reciprocal(inverse[:, 0:last], totals[:, 0:last])
+        quantise_w(1, "w_grouped0")
         scale(shares[0][:], 0)
         scale(shares[1][:], 1)
         nc.vector.reciprocal(inverse[:, last:SLOTS], totals[:, last:SLOTS])
@@ -166,7 +170,6 @@ def tile_picked_softkeys_none_p_kernel(
         scale(shares[3][:], 3)
         for t in (3, 0, 1, 2):
             scale(own_slots[:, t, :], t, HALF)
-        quantise_w(1, "exps2")
         for t in range(SLOTS):
             nc.sync.dma_start(late_slots[:, t, :], shares[t][:, HALF:S])
 
@@ -190,12 +193,11 @@ def tile_picked_softkeys_none_p_kernel(
             for b, (bank_tag, copy, queue) in enumerate(banks):
                 acc = psum.tile([P, per_bank, width], F32, name=f"acc{start}_{b}", tag=bank_tag)
                 for u in range(per_bank):
-                    half, block = divmod(per_bank * b + u, W_HALF // P)
-                    out_rows = slice(block * P, (block + 1) * P)
+                    block = per_bank * b + u
                     nc.tensor.matmul_mx(
                         out=acc[:, u, :],
-                        lhsT=w_codes[half][:, out_rows].bitcast(FP8X4),
-                        lhsT_scale=w_scales[half][:, out_rows],
+                        lhsT=w_codes[block][:].bitcast(FP8X4),
+                        lhsT_scale=w_scales[block][:],
                         rhs=z_codes[:].bitcast(FP8X4),
                         rhs_scale=z_scales[:],
                         start=True,
@@ -213,9 +215,11 @@ def tile_picked_softkeys_none_p_kernel(
         for t in range(last):
             fetch(fetched1[:, t, :], t, HALF, HALF, False)
         fetch(fetched1[:, last, :], last, HALF, HALF, False)
+        quantise_w(2, "exps2")
         grouped0 = group("grouped0", fetched0[:], 0, HALF, "grouped0")
+        quantise_w(3, "w_grouped2")
         multiply(grouped0[:], 0, HALF, [("bank4", nc.scalar.copy, nc.sync), ("bank5", nc.scalar.copy, nc.sync)])
-        late = keep.tile([P, HALF, SLOTS], BF16, name="late", tag="grouped0", align_bytes=64)
+        late = keep.tile([P, HALF, SLOTS], BF16, name="late", tag="w_grouped3", align_bytes=64)
         grouped1, grouped2 = late[:, 0:QUARTER, :], late[:, QUARTER:HALF, :]
         for part, start in ((grouped1, 0), (grouped2, QUARTER)):
             nc.vector.tensor_tensor(side_by_side(part, 2), by_slot(fetched1[:, :, start : start + QUARTER], 2), by_slot(late_slots[:, :, start : start + QUARTER], 2), ALU.add)

@@ -218,6 +218,16 @@ def tile_picked_softkeys_none_p_kernel(
         quantise_w(2, "exps2")
         grouped0 = group("grouped0", fetched0[:], 0, HALF, "grouped0")
         quantise_w(3, "w_grouped2")
+        unused = psum.tile([P, S], F32, name="unused", tag="bank1")
+        nc.tensor.matmul_mx(
+            out=unused[:],
+            lhsT=w_codes[3][:].bitcast(FP8X4),
+            lhsT_scale=w_scales[3][:],
+            rhs=query_words[:].bitcast(FP8X4),
+            rhs_scale=query_scales[:],
+            start=True,
+            stop=True,
+        )
         multiply(grouped0[:], 0, HALF, [("bank4", nc.scalar.copy, nc.sync), ("bank5", nc.scalar.copy, nc.sync)])
         late = keep.tile([P, HALF, SLOTS], BF16, name="late", tag="w_grouped3", align_bytes=64)
         grouped1, grouped2 = late[:, 0:QUARTER, :], late[:, QUARTER:HALF, :]

@@ -214,7 +214,8 @@ def tile_picked_softkeys_none_p_kernel(
             fetch(fetched0[:, t, :], t, 0, HALF, t == last)
         for t in range(last):
             fetch(fetched1[:, t, :], t, HALF, HALF, False)
-        fetch(fetched1[:, last, :], last, HALF, HALF, False)
+        fetch(fetched1[:, last, 0:QUARTER], last, HALF, QUARTER, False)
+        fetch(fetched1[:, last, QUARTER:HALF], last, HALF + QUARTER, QUARTER, False)
         quantise_w(2, "exps2")
         grouped0 = group("grouped0", fetched0[:], 0, HALF, "grouped0")
         quantise_w(3, "w_grouped2")

@@ -21,6 +21,7 @@ PER_COLUMN = 16
 QUADRANT = 32
 BLOCK = 8
 RUN = 4
+PAIR = 2
 SCORE_SCALE = 0.03125
 SHARE_SCALE = 32.0
 SCALE_ROWS = 4
@@ -137,12 +138,12 @@ def tile_picked_softkeys_none_p_kernel(
             nc.vector.tensor_scalar(negated[t][:], bank[:], -SCORE_SCALE, None, ALU.mult, ALU.min, accum_out=lowest[t][:])
 
         last = SLOTS - 1
-        totals = keep.tile([P, SLOTS], F32, name="totals", align_bytes=64)
+        totals = [keep.tile([P, PAIR], F32, name=f"totals{pair}", align_bytes=64) for pair in range(SLOTS // PAIR)]
         exps, shares = [], []
         for t in range(SLOTS):
             exps.append(keep.tile([P, S], F32, name=f"exps{t}", tag=f"exps{t}", align_bytes=64))
             shares.append(keep.tile([P, S], F32, name=f"shares{t}", align_bytes=64))
-            nc.scalar.activation(exps[t][:], negated[t][:], ACT.Exp, bias=lowest[t][:], scale=-1.0, accum_out=totals[:, t : t + 1])
+            nc.scalar.activation(exps[t][:], negated[t][:], ACT.Exp, bias=lowest[t][:], scale=-1.0, accum_out=totals[t // PAIR][:, t % PAIR : t % PAIR + 1])
 
         w_codes, w_scales = [], []
 
@@ -151,21 +152,21 @@ def tile_picked_softkeys_none_p_kernel(
             w_scales.append(keep.tile([P, P], U8, name=f"w_scales{half}", align_bytes=64))
             quantise(w_codes[half], w_scales[half], w_grouped[half][:])
 
-        inverse = keep.tile([P, SLOTS], F32, name="inverse", align_bytes=64)
+        inverse = [keep.tile([P, PAIR], F32, name=f"inverse{pair}", align_bytes=64) for pair in range(SLOTS // PAIR)]
         own = keep.tile([P, SLOTS * HALF], F32, name="own", align_bytes=64)
         own_slots = own[:].rearrange("p (t j) -> p t j", t=SLOTS)
         own_late = keep.tile([P, SLOTS * HALF], F32, name="own_late", align_bytes=64)
         late_slots = own_late[:].rearrange("p (t j) -> p t j", t=SLOTS)
 
         def scale(target, t, width=S):
-            nc.vector.tensor_scalar(target, exps[t][:, 0:width], inverse[:, t : t + 1], weight[:, t : t + 1], ALU.mult, ALU.mult)
+            nc.vector.tensor_scalar(target, exps[t][:, 0:width], inverse[t // PAIR][:, t % PAIR : t % PAIR + 1], weight[:, t : t + 1], ALU.mult, ALU.mult)
 
-        quantise_w(0, "x_word_table")
-        nc.vector.reciprocal(inverse[:, 0:last], totals[:, 0:last])
-        quantise_w(1, "w_grouped0")
+        nc.vector.reciprocal(inverse[0][:], totals[0][:])
+        quantise_w(0, "negated2")
         scale(shares[0][:], 0)
         scale(shares[1][:], 1)
-        nc.vector.reciprocal(inverse[:, last:SLOTS], totals[:, last:SLOTS])
+        nc.vector.reciprocal(inverse[1][:], totals[1][:])
+        quantise_w(1, "negated3")
         scale(shares[2][:], 2)
         scale(shares[3][:], 3)
         for t in (3, 0, 1, 2):
@@ -185,10 +186,14 @@ def tile_picked_softkeys_none_p_kernel(
             nc.vector.tensor_tensor(side_by_side(grouped[:], 2), by_slot(fetched, 2), by_slot(own_slots[:, :, start : start + width], 2), ALU.add)
             return grouped
 
-        def multiply(grouped, start, width, banks):
+        def quantise_z(grouped, start, width):
             z_codes = keep.tile([P, width], U32, name=f"z_codes{start}", align_bytes=64)
             z_scales = keep.tile([P, width], U8, name=f"z_scales{start}", align_bytes=64)
             quantise(z_codes, z_scales, grouped)
+            return z_codes, z_scales
+
+        def multiply(z, start, width, banks):
+            z_codes, z_scales = z
             per_bank = N // P // len(banks)
             for b, (bank_tag, copy, queue) in enumerate(banks):
                 acc = psum.tile([P, per_bank, width], F32, name=f"acc{start}_{b}", tag=bank_tag)
@@ -210,29 +215,34 @@ def tile_picked_softkeys_none_p_kernel(
 
         fetched0 = keep.tile([P, SLOTS, HALF], F32, name="fetched0", tag="fetched0", align_bytes=64)
         fetched1 = keep.tile([P, SLOTS, HALF], F32, name="fetched1", tag="exps3", align_bytes=64)
-        for t in range(SLOTS):
-            fetch(fetched0[:, t, :], t, 0, HALF, t == last)
+        for t in range(last):
+            fetch(fetched0[:, t, :], t, 0, HALF, False)
+        fetch(fetched0[:, last, 0:QUARTER], last, 0, QUARTER, True)
         for t in range(last):
             fetch(fetched1[:, t, :], t, HALF, HALF, False)
         fetch(fetched1[:, last, 0:QUARTER], last, HALF, QUARTER, False)
         fetch(fetched1[:, last, QUARTER:HALF], last, HALF + QUARTER, QUARTER, False)
         quantise_w(2, "exps2")
-        grouped0 = group("grouped0", fetched0[:], 0, HALF, "grouped0")
-        quantise_w(3, "w_grouped2")
         unused = psum.tile([P, S], F32, name="unused", tag="bank1")
         nc.tensor.matmul_mx(
             out=unused[:],
-            lhsT=w_codes[3][:].bitcast(FP8X4),
-            lhsT_scale=w_scales[3][:],
+            lhsT=w_codes[2][:].bitcast(FP8X4),
+            lhsT_scale=w_scales[2][:],
             rhs=query_words[:].bitcast(FP8X4),
             rhs_scale=query_scales[:],
             start=True,
             stop=True,
         )
-        multiply(grouped0[:], 0, HALF, [("bank4", nc.scalar.copy, nc.sync), ("bank5", nc.scalar.copy, nc.sync)])
+        grouped0 = group("grouped0", fetched0[:, :, 0:QUARTER], 0, QUARTER, "grouped0")
+        fetch(fetched0[:, last, QUARTER:HALF], last, QUARTER, QUARTER, True)
+        z0 = quantise_z(grouped0[:], 0, QUARTER)
+        grouped0b = group("grouped0b", fetched0[:, :, QUARTER:HALF], QUARTER, QUARTER, "grouped0b")
+        quantise_w(3, "grouped0")
+        multiply(z0, 0, QUARTER, [("bank4", nc.scalar.copy, nc.sync)])
+        multiply(quantise_z(grouped0b[:], QUARTER, QUARTER), QUARTER, QUARTER, [("bank5", nc.scalar.copy, nc.sync)])
         late = keep.tile([P, HALF, SLOTS], BF16, name="late", tag="w_grouped3", align_bytes=64)
         grouped1, grouped2 = late[:, 0:QUARTER, :], late[:, QUARTER:HALF, :]
         for part, start in ((grouped1, 0), (grouped2, QUARTER)):
             nc.vector.tensor_tensor(side_by_side(part, 2), by_slot(fetched1[:, :, start : start + QUARTER], 2), by_slot(late_slots[:, :, start : start + QUARTER], 2), ALU.add)
-        multiply(grouped1, HALF, QUARTER, [("bank6", nc.scalar.copy, nc.sync)])
-        multiply(grouped2, HALF + QUARTER, QUARTER, [("bank7", nc.vector.tensor_copy, nc.sync), ("bank0", nc.scalar.copy, nc.scalar)])
+        multiply(quantise_z(grouped1, HALF, QUARTER), HALF, QUARTER, [("bank6", nc.scalar.copy, nc.sync), ("bank2", nc.vector.tensor_copy, nc.sync)])
+        multiply(quantise_z(grouped2, HALF + QUARTER, QUARTER), HALF + QUARTER, QUARTER, [("bank7", nc.vector.tensor_copy, nc.sync), ("bank0", nc.scalar.copy, nc.scalar)])

@@ -95,7 +95,7 @@ def tile_picked_softkeys_none_p_kernel(
             nc.scalar.dma_start(w_halves[half], w_cols.rearrange("(p t) m -> p t m", t=SLOTS))
         weight = keep.tile([P, SLOTS], F32, name="weight", tag="d_word_table", align_bytes=64)
 
-        first_keys = keep.tile([P, P], U32, name="first_keys", tag="first_keys", align_bytes=64)
+        first_keys = keep.tile([P, PAIR, P], U32, name="first_keys", tag="first_keys", align_bytes=64)
         query_scales = keep.tile([P, S], U8, name="query_scales", align_bytes=64)
         query_words = keep.tile([P, S], U32, name="query_words", align_bytes=64)
         nc.vector.tensor_copy(query_scales[:], x_scale_table[:].indirect(offs_sb[:]))
@@ -109,33 +109,49 @@ def tile_picked_softkeys_none_p_kernel(
             columns = w_halves[1][:, :, u * P : (u + 1) * P].rearrange("p t c -> p c t")
             nc.gpsimd.tensor_scalar(w_grouped[2 + u][:], columns, 1.0, 0.0, ALU.mult, ALU.add)
         picked_by_slot = picked_words[:].rearrange("p (m t) -> p m t", t=SLOTS)
-        nc.vector.tensor_copy(first_keys[:], picked_by_slot[:, :, 0])
+        nc.vector.tensor_copy(first_keys[:].rearrange("p t m -> p m t"), picked_by_slot[:, :, 0:PAIR])
         halves = [slice(0, X_HALF), slice(X_HALF, S)]
         for cols in halves:
             nc.vector.tensor_copy(query_words[:, cols], x_word_table[:].indirect(entries(offs_sb, cols.start, X_HALF)))
-        other_keys = keep.tile([P, SLOTS - 1, P], U32, name="other_keys", tag="x_word_table", align_bytes=64)
-        nc.vector.tensor_copy(other_keys[:].rearrange("p t m -> p m t"), picked_by_slot[:, :, 1:SLOTS])
-        key_words = [first_keys[:]] + [other_keys[:, t, :] for t in range(SLOTS - 1)]
+        other_keys = keep.tile([P, PAIR, P], U32, name="other_keys", tag="x_word_table", align_bytes=64)
+        nc.vector.tensor_copy(other_keys[:].rearrange("p t m -> p m t"), picked_by_slot[:, :, PAIR:SLOTS])
+        key_words = [keys[:, t, :] for keys in (first_keys, other_keys) for t in range(PAIR)]
 
         def quantise(codes, scales, grouped):
             nc.vector.quantize_mx(out=codes[:].bitcast(FP8X4), scales=scales[:], in_=grouped.rearrange("p c t -> p (c t)"))
 
-        negated, lowest = [], []
-        for t in range(SLOTS):
-            bank = psum.tile([P, S], F32, name=f"scores{t}", tag=f"bank{t}")
-            for cols in halves if t == 0 else [slice(0, S)]:
-                nc.tensor.matmul_mx(
-                    out=bank[:, cols],
-                    lhsT=key_words[t].bitcast(FP8X4),
-                    lhsT_scale=key_scales[:, t * P : (t + 1) * P],
-                    rhs=query_words[:, cols].bitcast(FP8X4),
-                    rhs_scale=query_scales[:, cols],
-                    start=True,
-                    stop=True,
-                )
-            negated.append(keep.tile([P, S], F32, name=f"negated{t}", tag=f"negated{t}", align_bytes=64))
-            lowest.append(keep.tile([P, 1], F32, name=f"lowest{t}"))
-            nc.vector.tensor_scalar(negated[t][:], bank[:], -SCORE_SCALE, None, ALU.mult, ALU.min, accum_out=lowest[t][:])
+        w_codes, w_scales = [], []
+
+        def quantise_w(half, tag):
+            w_codes.append(keep.tile([P, P], U32, name=f"w_codes{half}", tag=tag, align_bytes=64))
+            w_scales.append(keep.tile([P, P], U8, name=f"w_scales{half}", align_bytes=64))
+            quantise(w_codes[half], w_scales[half], w_grouped[half][:])
+
+        quantise_w(0, "w_codes0")
+
+        negated = [keep.tile([P, S], F32, name=f"negated{t}", tag=f"negated{t}", align_bytes=64) for t in range(SLOTS)]
+        lowest = [keep.tile([P, 1], F32, name=f"lowest{t}") for t in range(SLOTS)]
+        lowest_early = [keep.tile([P, 1], F32, name=f"lowest_early{t}") for t in range(PAIR)]
+
+        def scores(t, cols, bank_tag, start_value, minimum):
+            bank = psum.tile([P, cols.stop - cols.start], F32, name=f"scores{t}_{cols.start}", tag=bank_tag)
+            nc.tensor.matmul_mx(
+                out=bank[:],
+                lhsT=key_words[t].bitcast(FP8X4),
+                lhsT_scale=key_scales[:, t * P : (t + 1) * P],
+                rhs=query_words[:, cols].bitcast(FP8X4),
+                rhs_scale=query_scales[:, cols],
+                start=True,
+                stop=True,
+            )
+            nc.vector.tensor_scalar(negated[t][:, cols], bank[:], -SCORE_SCALE, start_value, ALU.mult, ALU.min, accum_out=minimum)
+
+        for t in range(PAIR):
+            scores(t, halves[0], f"bank{SLOTS + t}", None, lowest_early[t][:])
+        for t in range(PAIR):
+            scores(t, halves[1], f"bank{t}", lowest_early[t][:], lowest[t][:])
+        for t in range(PAIR, SLOTS):
+            scores(t, slice(0, S), f"bank{t}", None, lowest[t][:])
 
         last = SLOTS - 1
         totals = [keep.tile([P, PAIR], F32, name=f"totals{pair}", align_bytes=64) for pair in range(SLOTS // PAIR)]
@@ -144,13 +160,6 @@ def tile_picked_softkeys_none_p_kernel(
             exps.append(keep.tile([P, S], F32, name=f"exps{t}", tag=f"exps{t}", align_bytes=64))
             shares.append(keep.tile([P, S], F32, name=f"shares{t}", align_bytes=64))
             nc.scalar.activation(exps[t][:], negated[t][:], ACT.Exp, bias=lowest[t][:], scale=-1.0, accum_out=totals[t // PAIR][:, t % PAIR : t % PAIR + 1])
-
-        w_codes, w_scales = [], []
-
-        def quantise_w(half, tag):
-            w_codes.append(keep.tile([P, P], U32, name=f"w_codes{half}", tag=tag, align_bytes=64))
-            w_scales.append(keep.tile([P, P], U8, name=f"w_scales{half}", align_bytes=64))
-            quantise(w_codes[half], w_scales[half], w_grouped[half][:])
 
         inverse = [keep.tile([P, PAIR], F32, name=f"inverse{pair}", align_bytes=64) for pair in range(SLOTS // PAIR)]
         own = keep.tile([P, SLOTS * HALF], F32, name="own", align_bytes=64)
@@ -162,11 +171,11 @@ def tile_picked_softkeys_none_p_kernel(
             nc.vector.tensor_scalar(target, exps[t][:, 0:width], inverse[t // PAIR][:, t % PAIR : t % PAIR + 1], weight[:, t : t + 1], ALU.mult, ALU.mult)
 
         nc.vector.reciprocal(inverse[0][:], totals[0][:])
-        quantise_w(0, "negated2")
+        quantise_w(1, "negated2")
         scale(shares[0][:], 0)
         scale(shares[1][:], 1)
         nc.vector.reciprocal(inverse[1][:], totals[1][:])
-        quantise_w(1, "negated3")
+        quantise_w(2, "negated3")
         scale(shares[2][:], 2)
         scale(shares[3][:], 3)
         for t in (3, 0, 1, 2):
@@ -218,29 +227,27 @@ def tile_picked_softkeys_none_p_kernel(
         for t in range(last):
             fetch(fetched0[:, t, :], t, 0, HALF, False)
         fetch(fetched0[:, last, 0:QUARTER], last, 0, QUARTER, True)
+        fetch(fetched0[:, last, QUARTER:HALF], last, QUARTER, QUARTER, True)
         for t in range(last):
             fetch(fetched1[:, t, :], t, HALF, HALF, False)
         fetch(fetched1[:, last, 0:QUARTER], last, HALF, QUARTER, False)
         fetch(fetched1[:, last, QUARTER:HALF], last, HALF + QUARTER, QUARTER, False)
-        quantise_w(2, "exps2")
+        quantise_w(3, "exps2")
         unused = psum.tile([P, S], F32, name="unused", tag="bank1")
         nc.tensor.matmul_mx(
             out=unused[:],
-            lhsT=w_codes[2][:].bitcast(FP8X4),
-            lhsT_scale=w_scales[2][:],
+            lhsT=w_codes[3][:].bitcast(FP8X4),
+            lhsT_scale=w_scales[3][:],
             rhs=query_words[:].bitcast(FP8X4),
             rhs_scale=query_scales[:],
             start=True,
             stop=True,
         )
         grouped0 = group("grouped0", fetched0[:, :, 0:QUARTER], 0, QUARTER, "grouped0")
-        fetch(fetched0[:, last, QUARTER:HALF], last, QUARTER, QUARTER, True)
-        z0 = quantise_z(grouped0[:], 0, QUARTER)
         grouped0b = group("grouped0b", fetched0[:, :, QUARTER:HALF], QUARTER, QUARTER, "grouped0b")
-        quantise_w(3, "grouped0")
-        multiply(z0, 0, QUARTER, [("bank4", nc.scalar.copy, nc.sync)])
+        multiply(quantise_z(grouped0[:], 0, QUARTER), 0, QUARTER, [("bank4", nc.scalar.copy, nc.sync)])
         multiply(quantise_z(grouped0b[:], QUARTER, QUARTER), QUARTER, QUARTER, [("bank5", nc.scalar.copy, nc.sync)])
-        late = keep.tile([P, HALF, SLOTS], BF16, name="late", tag="w_grouped3", align_bytes=64)
+        late = keep.tile([P, HALF, SLOTS], BF16, name="late", tag="grouped0", align_bytes=64)
         grouped1, grouped2 = late[:, 0:QUARTER, :], late[:, QUARTER:HALF, :]
         for part, start in ((grouped1, 0), (grouped2, QUARTER)):
             nc.vector.tensor_tensor(side_by_side(part, 2), by_slot(fetched1[:, :, start : start + QUARTER], 2), by_slot(late_slots[:, :, start : start + QUARTER], 2), ALU.add)

@@ -28,6 +28,7 @@ SCALE_ROWS = 4
 LEAD = 512
 X_PIECE_BYTES = 2048
 X_HALF = S // 2
+WARM_ROWS = 32
 W_HALF = N // 2
 HALF = S // 2
 QUARTER = S // 4
@@ -233,16 +234,17 @@ def tile_picked_softkeys_none_p_kernel(
         fetch(fetched1[:, last, 0:QUARTER], last, HALF, QUARTER, False)
         fetch(fetched1[:, last, QUARTER:HALF], last, HALF + QUARTER, QUARTER, False)
         quantise_w(3, "exps2")
-        unused = psum.tile([P, S], F32, name="unused", tag="bank1")
-        nc.tensor.matmul_mx(
-            out=unused[:],
-            lhsT=w_codes[3][:].bitcast(FP8X4),
-            lhsT_scale=w_scales[3][:],
-            rhs=query_words[:].bitcast(FP8X4),
-            rhs_scale=query_scales[:],
-            start=True,
-            stop=True,
-        )
+        for bank_tag in ("bank1", "bank3",):
+            unused = psum.tile([WARM_ROWS, S], F32, name="unused", tag=bank_tag)
+            nc.tensor.matmul_mx(
+                out=unused[:],
+                lhsT=w_codes[3][:, 0:WARM_ROWS].bitcast(FP8X4),
+                lhsT_scale=w_scales[3][:, 0:WARM_ROWS],
+                rhs=query_words[:].bitcast(FP8X4),
+                rhs_scale=query_scales[:],
+                start=True,
+                stop=True,
+            )
         grouped0 = group("grouped0", fetched0[:, :, 0:QUARTER], 0, QUARTER, "grouped0")
         grouped0b = group("grouped0b", fetched0[:, :, QUARTER:HALF], QUARTER, QUARTER, "grouped0b")
         multiply(quantise_z(grouped0[:], 0, QUARTER), 0, QUARTER, [("bank4", nc.scalar.copy, nc.sync)])

@@ -28,7 +28,6 @@ SCALE_ROWS = 4
 LEAD = 512
 X_PIECE_BYTES = 2048
 X_HALF = S // 2
-WARM_ROWS = 32
 W_HALF = N // 2
 HALF = S // 2
 QUARTER = S // 4
@@ -234,17 +233,6 @@ def tile_picked_softkeys_none_p_kernel(
         fetch(fetched1[:, last, 0:QUARTER], last, HALF, QUARTER, False)
         fetch(fetched1[:, last, QUARTER:HALF], last, HALF + QUARTER, QUARTER, False)
         quantise_w(3, "exps2")
-        for bank_tag in ("bank1", "bank3",):
-            unused = psum.tile([WARM_ROWS, S], F32, name="unused", tag=bank_tag)
-            nc.tensor.matmul_mx(
-                out=unused[:],
-                lhsT=w_codes[3][:, 0:WARM_ROWS].bitcast(FP8X4),
-                lhsT_scale=w_scales[3][:, 0:WARM_ROWS],
-                rhs=query_words[:].bitcast(FP8X4),
-                rhs_scale=query_scales[:],
-                start=True,
-                stop=True,
-            )
         grouped0 = group("grouped0", fetched0[:, :, 0:QUARTER], 0, QUARTER, "grouped0")
         grouped0b = group("grouped0b", fetched0[:, :, QUARTER:HALF], QUARTER, QUARTER, "grouped0b")
         multiply(quantise_z(grouped0[:], 0, QUARTER), 0, QUARTER, [("bank4", nc.scalar.copy, nc.sync)])

@@ -31,6 +31,7 @@ X_HALF = S // 2
 W_HALF = N // 2
 HALF = S // 2
 QUARTER = S // 4
+ON_VECTOR = 3 * QUARTER
 
 
 def side_by_side(grouped, run=RUN):
@@ -130,7 +131,7 @@ def tile_picked_softkeys_none_p_kernel(
         quantise_w(0, "w_codes0")
 
         negated = [keep.tile([P, S], F32, name=f"negated{t}", tag=f"negated{t}", align_bytes=64) for t in range(SLOTS)]
-        lowest = [keep.tile([P, 1], F32, name=f"lowest{t}") for t in range(SLOTS)]
+        lowest = [keep.tile([P, 1], F32, name=f"lowest{t}", tag=f"lowest{t}", align_bytes=64) for t in range(SLOTS)]
         lowest_early = [keep.tile([P, 1], F32, name=f"lowest_early{t}") for t in range(PAIR)]
 
         def scores(t, cols, bank_tag, start_value, minimum):
@@ -154,62 +155,68 @@ def tile_picked_softkeys_none_p_kernel(
             scores(t, slice(0, S), f"bank{t}", None, lowest[t][:])
 
         last = SLOTS - 1
-        totals = [keep.tile([P, PAIR], F32, name=f"totals{pair}", align_bytes=64) for pair in range(SLOTS // PAIR)]
-        exps, shares = [], []
+        groups = [range(0, last), range(last, SLOTS)]
+        totals = [keep.tile([P, len(g)], F32, name=f"totals{g.start}", align_bytes=64) for g in groups]
+        inverse = [keep.tile([P, len(g)], F32, name=f"inverse{g.start}", align_bytes=64) for g in groups]
+        factor = [keep.tile([P, len(g)], F32, name=f"factor{g.start}", align_bytes=64) for g in groups]
+
+        def column(tiles, t):
+            return tiles[t // last][:, t % last : t % last + 1]
+
+        exps = []
         for t in range(SLOTS):
-            exps.append(keep.tile([P, S], F32, name=f"exps{t}", tag=f"exps{t}", align_bytes=64))
-            shares.append(keep.tile([P, S], F32, name=f"shares{t}", align_bytes=64))
-            nc.scalar.activation(exps[t][:], negated[t][:], ACT.Exp, bias=lowest[t][:], scale=-1.0, accum_out=totals[t // PAIR][:, t % PAIR : t % PAIR + 1])
+            exps.append(keep.tile([P, S], F32, name=f"exps{t}", align_bytes=64))
+            nc.scalar.activation(exps[t][:], negated[t][:], ACT.Exp, bias=lowest[t][:], scale=-1.0, accum_out=column(totals, t))
 
-        inverse = [keep.tile([P, PAIR], F32, name=f"inverse{pair}", align_bytes=64) for pair in range(SLOTS // PAIR)]
-        own = keep.tile([P, SLOTS * HALF], F32, name="own", align_bytes=64)
-        own_slots = own[:].rearrange("p (t j) -> p t j", t=SLOTS)
-        own_late = keep.tile([P, SLOTS * HALF], F32, name="own_late", align_bytes=64)
-        late_slots = own_late[:].rearrange("p (t j) -> p t j", t=SLOTS)
+        own = keep.tile([P, SLOTS, S], F32, name="own", align_bytes=64)
+        fetched = [keep.tile([P, SLOTS, HALF], F32, name=f"fetched{half}", tag=tag, align_bytes=64) for half, tag in enumerate(("lowest3", "negated3"))]
+        unscaled = keep.tile([P, ON_VECTOR], F32, name="unscaled", tag="unscaled", align_bytes=64)
 
-        def scale(target, t, width=S):
-            nc.vector.tensor_scalar(target, exps[t][:, 0:width], inverse[t // PAIR][:, t % PAIR : t % PAIR + 1], weight[:, t : t + 1], ALU.mult, ALU.mult)
+        def scale(target, source, t):
+            nc.vector.tensor_scalar(target, source, column(inverse, t), weight[:, t : t + 1], ALU.mult, ALU.mult)
 
+        quantise_w(1, "negated1")
         nc.vector.reciprocal(inverse[0][:], totals[0][:])
-        quantise_w(1, "negated2")
-        scale(shares[0][:], 0)
-        scale(shares[1][:], 1)
+        quantise_w(2, "negated2")
+        nc.vector.tensor_tensor(factor[0][:], inverse[0][:], weight[:, 0:last], ALU.mult)
+        scale(own[:, 0, :], exps[0][:], 0)
         nc.vector.reciprocal(inverse[1][:], totals[1][:])
-        quantise_w(2, "negated3")
-        scale(shares[2][:], 2)
-        scale(shares[3][:], 3)
-        for t in (3, 0, 1, 2):
-            scale(own_slots[:, t, :], t, HALF)
-        for t in range(SLOTS):
-            nc.sync.dma_start(late_slots[:, t, :], shares[t][:, HALF:S])
+        scale(own[:, 1, :], exps[1][:], 1)
+        nc.vector.tensor_copy(unscaled[:], exps[last][:].indirect(entries(nb_sb, 0, ON_VECTOR)))
+        nc.vector.tensor_tensor(factor[1][:], inverse[1][:], weight[:, last:SLOTS], ALU.mult)
+        scale(own[:, 2, :], exps[2][:], 2)
+        scale(fetched[0][:, last, :], unscaled[:, 0:HALF], last)
+        scale(own[:, last, :], exps[last][:], last)
+        scale(fetched[1][:, last, 0 : ON_VECTOR - HALF], unscaled[:, HALF:ON_VECTOR], last)
 
-        def fetch(target, t, start, width, on_vector):
-            window = shares[t][:].indirect(entries(nb_sb, start, width))
-            if on_vector:
-                nc.vector.tensor_copy(target, window)
-            else:
-                nc.scalar.activation(target, window, ACT.Copy)
+        def fetch(t, start, width):
+            nc.scalar.activation(fetched[start // HALF][:, t, start % HALF : start % HALF + width], exps[t][:].indirect(entries(nb_sb, start, width)), ACT.Copy, scale=column(factor, t))
 
-        def group(name, fetched, start, width, tag):
-            grouped = keep.tile([P, width, SLOTS], BF16, name=name, tag=tag, align_bytes=64)
-            nc.vector.tensor_tensor(side_by_side(grouped[:], 2), by_slot(fetched, 2), by_slot(own_slots[:, :, start : start + width], 2), ALU.add)
-            return grouped
+        for start in (0, HALF):
+            for t in range(last):
+                fetch(t, start, HALF)
+        fetch(last, ON_VECTOR, S - ON_VECTOR)
 
-        def quantise_z(grouped, start, width):
-            z_codes = keep.tile([P, width], U32, name=f"z_codes{start}", align_bytes=64)
-            z_scales = keep.tile([P, width], U8, name=f"z_scales{start}", align_bytes=64)
+        def group(q, grouped):
+            cols = slice(q * QUARTER, (q + 1) * QUARTER)
+            nc.vector.tensor_tensor(side_by_side(grouped, 2), by_slot(fetched[q // 2][:, :, q % 2 * QUARTER : (q % 2 + 1) * QUARTER], 2), by_slot(own[:, :, cols], 2), ALU.add)
+
+        def quantise_z(grouped, q):
+            z_codes = keep.tile([P, QUARTER], U32, name=f"z_codes{q}", align_bytes=64)
+            z_scales = keep.tile([P, QUARTER], U8, name=f"z_scales{q}", align_bytes=64)
             quantise(z_codes, z_scales, grouped)
             return z_codes, z_scales
 
-        def multiply(z, start, width, banks):
+        def multiply(z, q, bank_tags):
             z_codes, z_scales = z
-            per_bank = N // P // len(banks)
-            for b, (bank_tag, copy, queue) in enumerate(banks):
-                acc = psum.tile([P, per_bank, width], F32, name=f"acc{start}_{b}", tag=bank_tag)
+            per_bank = N // P // len(bank_tags)
+            banks = []
+            for b, bank_tag in enumerate(bank_tags):
+                banks.append(psum.tile([P, per_bank, QUARTER], F32, name=f"acc{q}_{b}", tag=bank_tag))
                 for u in range(per_bank):
                     block = per_bank * b + u
                     nc.tensor.matmul_mx(
-                        out=acc[:, u, :],
+                        out=banks[b][:, u, :],
                         lhsT=w_codes[block][:].bitcast(FP8X4),
                         lhsT_scale=w_scales[block][:],
                         rhs=z_codes[:].bitcast(FP8X4),
@@ -217,29 +224,27 @@ def tile_picked_softkeys_none_p_kernel(
                         start=True,
                         stop=True,
                     )
-                result = keep.tile([P, per_bank, width], F32, name=f"result{start}_{b}", align_bytes=64)
-                copy(result[:], acc[:])
-                bank_rows = slice(per_bank * b * P, per_bank * (b + 1) * P)
-                queue.dma_start(out[bank_rows, start : start + width].rearrange("(u p) j -> p u j", p=P), result[:])
+            return banks
 
-        fetched0 = keep.tile([P, SLOTS, HALF], F32, name="fetched0", tag="fetched0", align_bytes=64)
-        fetched1 = keep.tile([P, SLOTS, HALF], F32, name="fetched1", tag="exps3", align_bytes=64)
-        for t in range(last):
-            fetch(fetched0[:, t, :], t, 0, HALF, False)
-        fetch(fetched0[:, last, 0:QUARTER], last, 0, QUARTER, True)
-        fetch(fetched0[:, last, QUARTER:HALF], last, QUARTER, QUARTER, True)
-        for t in range(last):
-            fetch(fetched1[:, t, :], t, HALF, HALF, False)
-        fetch(fetched1[:, last, 0:QUARTER], last, HALF, QUARTER, False)
-        fetch(fetched1[:, last, QUARTER:HALF], last, HALF + QUARTER, QUARTER, False)
-        quantise_w(3, "exps2")
-        grouped0 = group("grouped0", fetched0[:, :, 0:QUARTER], 0, QUARTER, "grouped0")
-        grouped0b = group("grouped0b", fetched0[:, :, QUARTER:HALF], QUARTER, QUARTER, "grouped0b")
-        multiply(quantise_z(grouped0[:], 0, QUARTER), 0, QUARTER, [("bank4", nc.scalar.copy, nc.sync)])
-        multiply(quantise_z(grouped0b[:], QUARTER, QUARTER), QUARTER, QUARTER, [("bank5", nc.scalar.copy, nc.sync)])
-        late = keep.tile([P, HALF, SLOTS], BF16, name="late", tag="grouped0", align_bytes=64)
-        grouped1, grouped2 = late[:, 0:QUARTER, :], late[:, QUARTER:HALF, :]
-        for part, start in ((grouped1, 0), (grouped2, QUARTER)):
-            nc.vector.tensor_tensor(side_by_side(part, 2), by_slot(fetched1[:, :, start : start + QUARTER], 2), by_slot(late_slots[:, :, start : start + QUARTER], 2), ALU.add)
-        multiply(quantise_z(grouped1, HALF, QUARTER), HALF, QUARTER, [("bank6", nc.scalar.copy, nc.sync), ("bank2", nc.vector.tensor_copy, nc.sync)])
-        multiply(quantise_z(grouped2, HALF + QUARTER, QUARTER), HALF + QUARTER, QUARTER, [("bank7", nc.vector.tensor_copy, nc.sync), ("bank0", nc.scalar.copy, nc.scalar)])
+        def store(banks, q, b, copy, queue):
+            per_bank = N // P // len(banks)
+            result = keep.tile([P, per_bank, QUARTER], F32, name=f"result{q}_{b}", align_bytes=64)
+            copy(result[:], banks[b][:])
+            bank_rows = slice(per_bank * b * P, per_bank * (b + 1) * P)
+            queue.dma_start(out[bank_rows, q * QUARTER : (q + 1) * QUARTER].rearrange("(u p) j -> p u j", p=P), result[:])
+
+        quantise_w(3, "unscaled")
+        early = [keep.tile([P, QUARTER, SLOTS], BF16, name=f"early{q}", tag=f"early{q}", align_bytes=64) for q in range(2)]
+        group(0, early[0][:])
+        group(1, early[1][:])
+        store(multiply(quantise_z(early[0][:], 0), 0, ["bank6"]), 0, 0, nc.scalar.copy, nc.sync)
+        store(multiply(quantise_z(early[1][:], 1), 1, ["bank7"]), 1, 0, nc.scalar.copy, nc.sync)
+        late = keep.tile([P, HALF, SLOTS], BF16, name="late", tag="early0", align_bytes=64)
+        group(2, late[:, 0:QUARTER, :])
+        group(3, late[:, QUARTER:HALF, :])
+        banks2 = multiply(quantise_z(late[:, 0:QUARTER, :], 2), 2, ["bank4", "bank1"])
+        store(banks2, 2, 0, nc.scalar.copy, nc.sync)
+        store(banks2, 2, 1, nc.vector.tensor_copy, nc.sync)
+        banks3 = multiply(quantise_z(late[:, QUARTER:HALF, :], 3), 3, ["bank5", "bank0"])
+        store(banks3, 3, 0, nc.vector.tensor_copy, nc.sync)
+        store(banks3, 3, 1, nc.scalar.copy, nc.scalar)

@@ -68,23 +68,23 @@ def tile_picked_softkeys_none_p_kernel(
 
         d_rows = d_words[0].rearrange("p n t -> p (n t)").bitcast(I32)
         nc.sync.dma_start(kidx_sb[:], kidx)
-        nc.sync.dma_start(d_word_table[:, 0:LEAD].bitcast(I32), d_rows[:, 0:LEAD])
+        nc.scalar.dma_start(d_word_table[:, 0:LEAD].bitcast(I32), d_rows[:, 0:LEAD])
+        nc.sync.dma_start(offs_sb[:], offs)
         nc.sync.dma_start(d_scale_table[0:P:BLOCK, :].bitcast(I32), d_scales[0].bitcast(I32))
         nc.sync.dma_start(d_word_table[:, LEAD:G].bitcast(I32), d_rows[:, LEAD:G])
-        nc.sync.dma_start(offs_sb[:], offs)
+        nc.sync.dma_start(nb_sb[:], nb)
         for a in range(SCALE_ROWS):
             rows = x_scales[0][a : P // BLOCK : SCALE_ROWS, :]
             nc.scalar.dma_start(x_scale_table[a:P:QUADRANT, :].bitcast(I32), rows.bitcast(I32))
         x_rows = x_words[0].rearrange("p n t -> p (n t)").bitcast(I32)
         nc.sync.dma_start(x_word_table[:].bitcast(I32), x_rows, max_dma_last_dim=X_PIECE_BYTES)
-        nc.sync.dma_start(nb_sb[:], nb)
         nc.gpsimd.dma_start(gn_sb[:], gn.rearrange("(p t) o -> p (t o)", t=SLOTS))
 
         picked_scales = keep.tile([P, H], U8, name="picked_scales", tag="picked_scales", align_bytes=64)
         key_scales = keep.tile([P, H], U8, name="key_scales", align_bytes=64)
         nc.vector.tensor_copy(picked_scales[:], d_scale_table[:].indirect(kidx_sb[:]))
         nc.vector.tensor_copy(
-            key_scales[:].rearrange("p (t m) -> p m t", t=SLOTS), picked_scales[:].rearrange("p (m t) -> p m t", t=SLOTS)
+            key_scales[:].rearrange("p (t m) -> p t m", t=SLOTS), picked_scales[:].rearrange("p (m t) -> p t m", t=SLOTS)
         )
         for a in range(1, SCALE_ROWS):
             nc.scalar.dma_start(key_scales[a:P:QUADRANT, :].bitcast(I32), key_scales[BLOCK * a : P : QUADRANT, :].bitcast(I32))
@@ -96,12 +96,12 @@ def tile_picked_softkeys_none_p_kernel(
             nc.scalar.dma_start(w_halves[half], w_cols.rearrange("(p t) m -> p t m", t=SLOTS))
         weight = keep.tile([P, SLOTS], F32, name="weight", tag="d_word_table", align_bytes=64)
 
-        first_keys = keep.tile([P, PAIR, P], U32, name="first_keys", tag="first_keys", align_bytes=64)
+        keys = keep.tile([P, SLOTS, P], U32, name="keys", align_bytes=64)
         query_scales = keep.tile([P, S], U8, name="query_scales", align_bytes=64)
         query_words = keep.tile([P, S], U32, name="query_words", align_bytes=64)
-        nc.vector.tensor_copy(query_scales[:], x_scale_table[:].indirect(offs_sb[:]))
         picked_words = keep.tile([P, H], U32, name="picked_words", align_bytes=64)
         nc.vector.tensor_copy(picked_words[:], d_word_table[:].indirect(kidx_sb[:]))
+        nc.vector.tensor_copy(query_scales[:], x_scale_table[:].indirect(offs_sb[:]))
         nc.scalar.activation(weight[:], gn_sb[:], ACT.Copy, scale=SHARE_SCALE)
         w_grouped = [keep.tile([P, P, SLOTS], BF16, name=f"w_grouped{u}", tag=f"w_grouped{u}", align_bytes=64) for u in range(N // P)]
         for u in range(2):
@@ -110,13 +110,11 @@ def tile_picked_softkeys_none_p_kernel(
             columns = w_halves[1][:, :, u * P : (u + 1) * P].rearrange("p t c -> p c t")
             nc.gpsimd.tensor_scalar(w_grouped[2 + u][:], columns, 1.0, 0.0, ALU.mult, ALU.add)
         picked_by_slot = picked_words[:].rearrange("p (m t) -> p m t", t=SLOTS)
-        nc.vector.tensor_copy(first_keys[:].rearrange("p t m -> p m t"), picked_by_slot[:, :, 0:PAIR])
+        nc.vector.tensor_copy(keys[:].rearrange("p t m -> p m t"), picked_by_slot)
         halves = [slice(0, X_HALF), slice(X_HALF, S)]
         for cols in halves:
             nc.vector.tensor_copy(query_words[:, cols], x_word_table[:].indirect(entries(offs_sb, cols.start, X_HALF)))
-        other_keys = keep.tile([P, PAIR, P], U32, name="other_keys", tag="x_word_table", align_bytes=64)
-        nc.vector.tensor_copy(other_keys[:].rearrange("p t m -> p m t"), picked_by_slot[:, :, PAIR:SLOTS])
-        key_words = [keys[:, t, :] for keys in (first_keys, other_keys) for t in range(PAIR)]
+        key_words = [keys[:, t, :] for t in range(SLOTS)]
 
         def quantise(codes, scales, grouped):
             nc.vector.quantize_mx(out=codes[:].bitcast(FP8X4), scales=scales[:], in_=grouped.rearrange("p c t -> p (c t)"))
@@ -237,8 +235,10 @@ def tile_picked_softkeys_none_p_kernel(
         early = [keep.tile([P, QUARTER, SLOTS], BF16, name=f"early{q}", tag=f"early{q}", align_bytes=64) for q in range(2)]
         group(0, early[0][:])
         group(1, early[1][:])
-        store(multiply(quantise_z(early[0][:], 0), 0, ["bank6"]), 0, 0, nc.scalar.copy, nc.sync)
-        store(multiply(quantise_z(early[1][:], 1), 1, ["bank7"]), 1, 0, nc.scalar.copy, nc.sync)
+        for q, bank_tags in enumerate((["bank6", "bank2"], ["bank7", "bank3"])):
+            banks = multiply(quantise_z(early[q][:], q), q, bank_tags)
+            for b in range(2):
+                store(banks, q, b, nc.scalar.copy, nc.sync)
         late = keep.tile([P, HALF, SLOTS], BF16, name="late", tag="early0", align_bytes=64)
         group(2, late[:, 0:QUARTER, :])
         group(3, late[:, QUARTER:HALF, :])

from contextlib import ExitStack

import concourse.mybir as mybir

F32 = mybir.dt.float32
BF16 = mybir.dt.bfloat16
I32 = mybir.dt.int32
U32 = mybir.dt.uint32
U16 = mybir.dt.uint16
U8 = mybir.dt.uint8
FP8X4 = mybir.dt.float8_e4m3fn_x4
ALU = mybir.AluOpType
ACT = mybir.ActivationFunctionType

K, T, S, N, G, H = 512, 2048, 512, 512, 2048, 512
FLOPS = 2 * K * H * S + 2 * H * N * S

P = 128
SLOTS = 4
PER_COLUMN = 16
QUADRANT = 32
BLOCK = 8
RUN = 4
PAIR = 2
SCORE_SCALE = 0.03125
SHARE_SCALE = 32.0
SCALE_ROWS = 4
LEAD = 512
X_PIECE_BYTES = 2048
X_HALF = S // 2
W_HALF = N // 2
HALF = S // 2
QUARTER = S // 4
ON_VECTOR = 3 * QUARTER


def side_by_side(grouped, run=RUN):
    return grouped.rearrange("p (c i) t -> p c t i", i=run)


def by_slot(planes, run=RUN):
    return planes.rearrange("p t (c i) -> p c t i", i=run)


def entries(offsets, start, count):
    return offsets[:, start // PER_COLUMN : (start + count) // PER_COLUMN]


def tile_picked_softkeys_none_p_kernel(
    tc, x_words, x_scales, d_words, d_scales, gn, w1, offs, kidx, nb, out
):
    nc = tc.nc
    with ExitStack() as ctx:
        keep = ctx.enter_context(tc.tile_pool(name="keep", bufs=1))
        psum = ctx.enter_context(tc.psum_pool(name="psum", bufs=1))

        kidx_sb = keep.tile([P, H // PER_COLUMN], U16, name="kidx_sb")
        offs_sb = keep.tile([P, S // PER_COLUMN], U16, name="offs_sb")
        nb_sb = keep.tile([P, S // PER_COLUMN], U16, name="nb_sb")
        d_scale_table = keep.tile([P, G], U8, name="d_scale_table", align_bytes=64)
        x_scale_table = keep.tile([P, T], U8, name="x_scale_table", align_bytes=64)
        d_word_table = keep.tile([P, G], U32, name="d_word_table", tag="d_word_table", align_bytes=64)
        x_word_table = keep.tile([P, T], U32, name="x_word_table", tag="x_word_table", align_bytes=64)
        gn_sb = keep.tile([P, SLOTS], F32, name="gn_sb")

        nc.vector.memset(d_scale_table[:].bitcast(I32), 0)
        nc.vector.memset(x_scale_table[:].bitcast(I32), 0)

        d_rows = d_words[0].rearrange("p n t -> p (n t)").bitcast(I32)
        nc.sync.dma_start(kidx_sb[:], kidx)
        nc.scalar.dma_start(d_word_table[:, 0:LEAD].bitcast(I32), d_rows[:, 0:LEAD])
        nc.sync.dma_start(offs_sb[:], offs)
        nc.sync.dma_start(d_scale_table[0:P:BLOCK, :].bitcast(I32), d_scales[0].bitcast(I32))
        nc.sync.dma_start(d_word_table[:, LEAD:G].bitcast(I32), d_rows[:, LEAD:G])
        nc.sync.dma_start(nb_sb[:], nb)
        for a in range(SCALE_ROWS):
            rows = x_scales[0][a : P // BLOCK : SCALE_ROWS, :]
            nc.scalar.dma_start(x_scale_table[a:P:QUADRANT, :].bitcast(I32), rows.bitcast(I32))
        x_rows = x_words[0].rearrange("p n t -> p (n t)").bitcast(I32)
        nc.sync.dma_start(x_word_table[:].bitcast(I32), x_rows, max_dma_last_dim=X_PIECE_BYTES)
        nc.gpsimd.dma_start(gn_sb[:], gn.rearrange("(p t) o -> p (t o)", t=SLOTS))

        picked_scales = keep.tile([P, H], U8, name="picked_scales", tag="picked_scales", align_bytes=64)
        key_scales = keep.tile([P, H], U8, name="key_scales", align_bytes=64)
        nc.vector.tensor_copy(picked_scales[:], d_scale_table[:].indirect(kidx_sb[:]))
        nc.vector.tensor_copy(
            key_scales[:].rearrange("p (t m) -> p t m", t=SLOTS), picked_scales[:].rearrange("p (m t) -> p t m", t=SLOTS)
        )
        for a in range(1, SCALE_ROWS):
            nc.scalar.dma_start(key_scales[a:P:QUADRANT, :].bitcast(I32), key_scales[BLOCK * a : P : QUADRANT, :].bitcast(I32))

        w_raw = keep.tile([P, 2 * SLOTS * W_HALF], F32, name="w_raw", tag="picked_scales", align_bytes=64)
        w_halves = [w_raw[:, half * SLOTS * W_HALF : (half + 1) * SLOTS * W_HALF].rearrange("p (t m) -> p t m", t=SLOTS) for half in range(2)]
        for half in range(2):
            w_cols = w1[:, half * W_HALF : (half + 1) * W_HALF]
            nc.scalar.dma_start(w_halves[half], w_cols.rearrange("(p t) m -> p t m", t=SLOTS))
        weight = keep.tile([P, SLOTS], F32, name="weight", tag="d_word_table", align_bytes=64)

        keys = keep.tile([P, SLOTS, P], U32, name="keys", align_bytes=64)
        query_scales = keep.tile([P, S], U8, name="query_scales", align_bytes=64)
        query_words = keep.tile([P, S], U32, name="query_words", align_bytes=64)
        picked_words = keep.tile([P, H], U32, name="picked_words", align_bytes=64)
        nc.vector.tensor_copy(picked_words[:], d_word_table[:].indirect(kidx_sb[:]))
        nc.vector.tensor_copy(query_scales[:], x_scale_table[:].indirect(offs_sb[:]))
        nc.scalar.activation(weight[:], gn_sb[:], ACT.Copy, scale=SHARE_SCALE)
        w_grouped = [keep.tile([P, P, SLOTS], BF16, name=f"w_grouped{u}", tag=f"w_grouped{u}", align_bytes=64) for u in range(N // P)]
        for u in range(2):
            nc.scalar.copy(side_by_side(w_grouped[u][:]), by_slot(w_halves[0][:, :, u * P : (u + 1) * P]))
        for u in range(2):
            columns = w_halves[1][:, :, u * P : (u + 1) * P].rearrange("p t c -> p c t")
            nc.gpsimd.tensor_scalar(w_grouped[2 + u][:], columns, 1.0, 0.0, ALU.mult, ALU.add)
        picked_by_slot = picked_words[:].rearrange("p (m t) -> p m t", t=SLOTS)
        nc.vector.tensor_copy(keys[:].rearrange("p t m -> p m t"), picked_by_slot)
        halves = [slice(0, X_HALF), slice(X_HALF, S)]
        for cols in halves:
            nc.vector.tensor_copy(query_words[:, cols], x_word_table[:].indirect(entries(offs_sb, cols.start, X_HALF)))
        key_words = [keys[:, t, :] for t in range(SLOTS)]

        def quantise(codes, scales, grouped):
            nc.vector.quantize_mx(out=codes[:].bitcast(FP8X4), scales=scales[:], in_=grouped.rearrange("p c t -> p (c t)"))

        w_codes, w_scales = [], []

        def quantise_w(half, tag):
            w_codes.append(keep.tile([P, P], U32, name=f"w_codes{half}", tag=tag, align_bytes=64))
            w_scales.append(keep.tile([P, P], U8, name=f"w_scales{half}", align_bytes=64))
            quantise(w_codes[half], w_scales[half], w_grouped[half][:])

        quantise_w(0, "w_codes0")

        negated = [keep.tile([P, S], F32, name=f"negated{t}", tag=f"negated{t}", align_bytes=64) for t in range(SLOTS)]
        lowest = [keep.tile([P, 1], F32, name=f"lowest{t}", tag=f"lowest{t}", align_bytes=64) for t in range(SLOTS)]
        lowest_early = [keep.tile([P, 1], F32, name=f"lowest_early{t}") for t in range(PAIR)]

        def scores(t, cols, bank_tag, start_value, minimum):
            bank = psum.tile([P, cols.stop - cols.start], F32, name=f"scores{t}_{cols.start}", tag=bank_tag)
            nc.tensor.matmul_mx(
                out=bank[:],
                lhsT=key_words[t].bitcast(FP8X4),
                lhsT_scale=key_scales[:, t * P : (t + 1) * P],
                rhs=query_words[:, cols].bitcast(FP8X4),
                rhs_scale=query_scales[:, cols],
                start=True,
                stop=True,
            )
            nc.vector.tensor_scalar(negated[t][:, cols], bank[:], -SCORE_SCALE, start_value, ALU.mult, ALU.min, accum_out=minimum)

        for t in range(PAIR):
            scores(t, halves[0], f"bank{SLOTS + t}", None, lowest_early[t][:])
        for t in range(PAIR):
            scores(t, halves[1], f"bank{t}", lowest_early[t][:], lowest[t][:])
        for t in range(PAIR, SLOTS):
            scores(t, slice(0, S), f"bank{t}", None, lowest[t][:])

        last = SLOTS - 1
        groups = [range(0, last), range(last, SLOTS)]
        totals = [keep.tile([P, len(g)], F32, name=f"totals{g.start}", align_bytes=64) for g in groups]
        inverse = [keep.tile([P, len(g)], F32, name=f"inverse{g.start}", align_bytes=64) for g in groups]
        factor = [keep.tile([P, len(g)], F32, name=f"factor{g.start}", align_bytes=64) for g in groups]

        def column(tiles, t):
            return tiles[t // last][:, t % last : t % last + 1]

        exps = []
        for t in range(SLOTS):
            exps.append(keep.tile([P, S], F32, name=f"exps{t}", align_bytes=64))
            nc.scalar.activation(exps[t][:], negated[t][:], ACT.Exp, bias=lowest[t][:], scale=-1.0, accum_out=column(totals, t))

        own = keep.tile([P, SLOTS, S], F32, name="own", align_bytes=64)
        fetched = [keep.tile([P, SLOTS, HALF], F32, name=f"fetched{half}", tag=tag, align_bytes=64) for half, tag in enumerate(("lowest3", "negated3"))]
        unscaled = keep.tile([P, ON_VECTOR], F32, name="unscaled", tag="unscaled", align_bytes=64)

        def scale(target, source, t):
            nc.vector.tensor_scalar(target, source, column(inverse, t), weight[:, t : t + 1], ALU.mult, ALU.mult)

        quantise_w(1, "negated1")
        nc.vector.reciprocal(inverse[0][:], totals[0][:])
        quantise_w(2, "negated2")
        nc.vector.tensor_tensor(factor[0][:], inverse[0][:], weight[:, 0:last], ALU.mult)
        scale(own[:, 0, :], exps[0][:], 0)
        nc.vector.reciprocal(inverse[1][:], totals[1][:])
        scale(own[:, 1, :], exps[1][:], 1)
        nc.vector.tensor_copy(unscaled[:], exps[last][:].indirect(entries(nb_sb, 0, ON_VECTOR)))
        nc.vector.tensor_tensor(factor[1][:], inverse[1][:], weight[:, last:SLOTS], ALU.mult)
        scale(own[:, 2, :], exps[2][:], 2)
        scale(fetched[0][:, last, :], unscaled[:, 0:HALF], last)
        scale(own[:, last, :], exps[last][:], last)
        scale(fetched[1][:, last, 0 : ON_VECTOR - HALF], unscaled[:, HALF:ON_VECTOR], last)

        def fetch(t, start, width):
            nc.scalar.activation(fetched[start // HALF][:, t, start % HALF : start % HALF + width], exps[t][:].indirect(entries(nb_sb, start, width)), ACT.Copy, scale=column(factor, t))

        for start in (0, HALF):
            for t in range(last):
                fetch(t, start, HALF)
        fetch(last, ON_VECTOR, S - ON_VECTOR)

        def group(q, grouped):
            cols = slice(q * QUARTER, (q + 1) * QUARTER)
            nc.vector.tensor_tensor(side_by_side(grouped, 2), by_slot(fetched[q // 2][:, :, q % 2 * QUARTER : (q % 2 + 1) * QUARTER], 2), by_slot(own[:, :, cols], 2), ALU.add)

        def quantise_z(grouped, q):
            z_codes = keep.tile([P, QUARTER], U32, name=f"z_codes{q}", align_bytes=64)
            z_scales = keep.tile([P, QUARTER], U8, name=f"z_scales{q}", align_bytes=64)
            quantise(z_codes, z_scales, grouped)
            return z_codes, z_scales

        def multiply(z, q, bank_tags):
            z_codes, z_scales = z
            per_bank = N // P // len(bank_tags)
            banks = []
            for b, bank_tag in enumerate(bank_tags):
                banks.append(psum.tile([P, per_bank, QUARTER], F32, name=f"acc{q}_{b}", tag=bank_tag))
                for u in range(per_bank):
                    block = per_bank * b + u
                    nc.tensor.matmul_mx(
                        out=banks[b][:, u, :],
                        lhsT=w_codes[block][:].bitcast(FP8X4),
                        lhsT_scale=w_scales[block][:],
                        rhs=z_codes[:].bitcast(FP8X4),
                        rhs_scale=z_scales[:],
                        start=True,
                        stop=True,
                    )
            return banks

        def store(banks, q, b, copy, queue):
            per_bank = N // P // len(banks)
            result = keep.tile([P, per_bank, QUARTER], F32, name=f"result{q}_{b}", align_bytes=64)
            copy(result[:], banks[b][:])
            bank_rows = slice(per_bank * b * P, per_bank * (b + 1) * P)
            queue.dma_start(out[bank_rows, q * QUARTER : (q + 1) * QUARTER].rearrange("(u p) j -> p u j", p=P), result[:])

        quantise_w(3, "unscaled")
        early = [keep.tile([P, QUARTER, SLOTS], BF16, name=f"early{q}", tag=f"early{q}", align_bytes=64) for q in range(2)]
        group(0, early[0][:])
        group(1, early[1][:])
        for q, bank_tags in enumerate((["bank6", "bank2"], ["bank7", "bank3"])):
            banks = multiply(quantise_z(early[q][:], q), q, bank_tags)
            for b in range(2):
                store(banks, q, b, nc.scalar.copy, nc.sync)
        late = keep.tile([P, HALF, SLOTS], BF16, name="late", tag="early0", align_bytes=64)
        group(2, late[:, 0:QUARTER, :])
        group(3, late[:, QUARTER:HALF, :])
        banks2 = multiply(quantise_z(late[:, 0:QUARTER, :], 2), 2, ["bank4", "bank1"])
        store(banks2, 2, 0, nc.scalar.copy, nc.sync)
        store(banks2, 2, 1, nc.vector.tensor_copy, nc.sync)
        banks3 = multiply(quantise_z(late[:, QUARTER:HALF, :], 3), 3, ["bank5", "bank0"])
        store(banks3, 3, 0, nc.vector.tensor_copy, nc.sync)
        store(banks3, 3, 1, nc.scalar.copy, nc.scalar)
